import numpy as np
import ml_dtypes


def mxq(x, axis, fmt="e4m3"):
    dtype, down = {"e4m3": (ml_dtypes.float8_e4m3fn, 7), "e5m2": (ml_dtypes.float8_e5m2, 14)}[fmt]
    v = np.moveaxis(np.asarray(x, np.float32).astype(ml_dtypes.bfloat16).astype(np.float64), axis, -1)
    blocks = v.reshape(v.shape[:-1] + (-1, 32))
    amax = np.abs(blocks).max(-1, keepdims=True)
    byte = np.maximum(np.where(amax > 0, np.frexp(amax)[1] - 1 + 127, 0) - down, 1)
    scale = np.exp2(byte - 127.0)
    codes = (blocks / scale).astype(np.float32).astype(dtype).astype(np.float64)
    return np.moveaxis((codes * scale).reshape(v.shape), -1, axis)


WIDE = False


def mx_kscale(k):
    if not WIDE:
        return np.ones(k)
    levels = np.array([10, -10, 5, -5, 0])
    if k % 512:
        return np.exp2(np.random.permutation(np.resize(levels, k // 32))).repeat(32)
    a = np.empty((k // 512, 16))
    for p in range(k // 512):
        a[p, :8] = np.random.permutation(np.resize(levels, 8))
        for g in range(8):
            far = levels[np.abs(levels - a[p, g]) >= 10]
            a[p, g + 8] = far[np.random.randint(len(far))]
    return np.exp2(a.ravel()).repeat(32)


def f64(x):
    return np.asarray(x).astype(np.float64)


def striped(idx):
    return np.tile(idx.reshape(-1, 16).T, (8, 1)).astype(np.uint16)


def unstriped(offs):
    return offs[:16].T.reshape(-1).astype(np.int64)


def pack_weight(w):
    k, n = w.shape
    w = f64(np.asarray(w, np.float32).astype(ml_dtypes.bfloat16)).reshape(k // 32, 32, n)
    amax = np.abs(w).max(1)
    byte = np.clip(np.where(amax > 0, np.frexp(amax)[1] - 1 + 127 - 7, 1), 1, 254)
    scaled = (w * np.exp2(127.0 - byte)[:, None, :]).reshape(k, n).astype(np.float32)
    words = np.ascontiguousarray(scaled.reshape(k // 512, 128, 4, n).transpose(0, 1, 3, 2)).astype(ml_dtypes.float8_e4m3fn).view(np.uint8)
    return words, np.ascontiguousarray(byte.astype(np.uint8).reshape(k // 512, 16, n))


def unpack_weight(words, scales):
    g, p, n, _ = words.shape
    vals = np.ascontiguousarray(words).view(ml_dtypes.float8_e4m3fn).astype(np.float64) * np.repeat(np.exp2(scales.astype(np.float64) - 127.0), 8, axis=1)[..., None]
    return vals.transpose(0, 1, 3, 2).reshape(g * 512, n)


def relu(v):
    return np.maximum(v, 0.0)


K, T, S, V, H, N = 1024, 1024, 512, 256, 512, 256


def setup_inputs():
    n = np.random.standard_normal
    s = mx_kscale(K)[:, None]
    u = mx_kscale(H)
    packed_w2 = pack_weight(n((H, N)) / np.sqrt(2 * H) / u[:, None])
    packed_w3 = pack_weight(n((H, N)) / np.sqrt(2 * H) / u[:, None])
    return {
        "xT": (n((K, T)) * s).astype(np.float32),
        "w1": (n((K, H)) / np.sqrt(K) / s * u).astype(np.float32),
        "w2_words": packed_w2[0],
        "w2_scales": packed_w2[1],
        "w3_words": packed_w3[0],
        "w3_scales": packed_w3[1],
        "offs": striped(np.random.permutation(T)[:S]),
        "cen": striped(np.random.permutation(S)[:V]),
        "pos1": striped(np.random.permutation(S)[:V]),
        "pos2": striped(np.random.permutation(S)[:V]),
    }


def reference(xT, w1, w2_words, w2_scales, w3_words, w3_scales, offs, cen, pos1, pos2):
    xq = mxq(f64(xT)[:, unstriped(offs)], 0, "e4m3")
    h = relu(mxq(f64(w1), 0, "e4m3").T @ xq)
    hc = h[:, unstriped(cen)]
    z = np.maximum(h[:, unstriped(pos1)], h[:, unstriped(pos2)])
    return unpack_weight(w2_words, w2_scales).T @ mxq(hc, 0, "e4m3") + unpack_weight(w3_words, w3_scales).T @ mxq(z, 0, "e4m3")

@@ -1,0 +1,180 @@
+from contextlib import ExitStack
+
+import concourse.mybir as mybir
+
+K, T, S, V, H, N = 1024, 1024, 512, 256, 512, 256
+FLOPS = 2 * K * H * S + 2 * 2 * H * N * V
+
+F32 = mybir.dt.float32
+BF16 = mybir.dt.bfloat16
+I32 = mybir.dt.int32
+U32 = mybir.dt.uint32
+U16 = mybir.dt.uint16
+U8 = mybir.dt.uint8
+FP8X4 = mybir.dt.float8_e4m3fn_x4
+COPY = mybir.ActivationFunctionType.Copy
+RELU = mybir.ActivationFunctionType.Relu
+MAX = mybir.AluOpType.max
+
+P = 128
+PACK = 4
+K_PASS = P * PACK
+PASSES = K // K_PASS
+
+X_CHUNKS = [
+    [(0, 256, 128), (256, 256, 128), (512, 512, 320)],
+    [(0, 256, 0), (256, 256, 0), (512, 256, 0), (768, 128, 0), (896, 128, 80)],
+]
+W_CHUNKS = [[(0, 256, 0), (256, 256, 0)], [(0, 192, 0), (192, 192, 0), (384, 128, 0)]]
+CEN_VECTOR = 168
+
+
+def tile_picked_sagecat_max_e_kernel(tc, xT, w1, w2_words, w2_scales, w3_words, w3_scales, offs, cen, pos1, pos2, out):
+    nc = tc.nc
+    with ExitStack() as ctx:
+        keep = ctx.enter_context(tc.tile_pool(name="keep", bufs=1))
+        psum = ctx.enter_context(tc.psum_pool(name="psum", bufs=1))
+
+        def sb(shape, dtype, name):
+            return keep.tile(shape, dtype, name=name, align_bytes=64)
+
+        offs_sb = sb([P, S // 16], U16, "offs_sb")
+        cen_sb = sb([P, V // 16], U16, "cen_sb")
+        pos1_sb = sb([P, V // 16], U16, "pos1_sb")
+        pos2_sb = sb([P, V // 16], U16, "pos2_sb")
+
+        x_scales = [sb([P, T], U8, f"x_scales{g}") for g in range(PASSES)]
+        for g in range(PASSES):
+            nc.vector.memset(x_scales[g][:].bitcast(I32), 0)
+        w23_scales = [sb([P, N], U8, f"w23_scales{a}") for a in range(2)]
+        for a in range(2):
+            nc.vector.memset(w23_scales[a][:].bitcast(I32), 0)
+
+        x_raw, w_raw = {}, {}
+        for g in range(PASSES):
+            for src, chunks, raws, label in ((xT, X_CHUNKS, x_raw, "x"), (w1, W_CHUNKS, w_raw, "w")):
+                rows = src[g * K_PASS : (g + 1) * K_PASS, :].rearrange("(p j) c -> p j c", j=PACK)
+                for c0, width, share in chunks[g]:
+                    raws[g, c0] = sb([P, PACK, width], F32, f"{label}_raw{g}_{c0}")
+                    nc.sync.dma_start(out=raws[g, c0][:], in_=rows[:, :, c0 : c0 + width])
+                if g == 0 and label == "x":
+                    nc.sync.dma_start(offs_sb[:], offs)
+        nc.sync.dma_start(pos1_sb[:], pos1)
+        nc.sync.dma_start(pos2_sb[:], pos2)
+        nc.sync.dma_start(cen_sb[:], cen)
+        w23_words = [sb([P, N], U32, f"w23_words{a}") for a in range(2)]
+        for a, (words, scales) in enumerate(((w3_words, w3_scales), (w2_words, w2_scales))):
+            nc.sync.dma_start(out=w23_words[a][:].bitcast(I32), in_=words[0].rearrange("p n t -> p (n t)").bitcast(I32))
+            for q in range(4):
+                nc.sync.dma_start(
+                    out=w23_scales[a][32 * q : 32 * q + 4, :].bitcast(I32),
+                    in_=scales[0, 4 * q : 4 * q + 4, :].bitcast(I32),
+                )
+
+        x_words = [sb([P, T], U32, f"x_words{g}") for g in range(PASSES)]
+        xg_words = [sb([P, S], U32, f"xg_words{g}") for g in range(PASSES)]
+        xg_scales = [sb([P, S], U8, f"xg_scales{g}") for g in range(PASSES)]
+        w_bf = [sb([P, H * PACK], BF16, f"w_bf{g}") for g in range(PASSES)]
+        w_words = [sb([P, H], U32, f"w_words{g}") for g in range(PASSES)]
+        w_scales = [sb([P, H], U8, f"w_scales{g}") for g in range(PASSES)]
+        pieces = [(0, 0, S // 2), (0, S // 2, S // 2)] + [(t, 0, S) for t in range(1, PACK)]
+        h_ps = [psum.tile([P, width], F32, name=f"h_ps{n}") for n, (t, s0, width) in enumerate(pieces)]
+        h = [sb([P, S], F32, f"h{t}") for t in range(PACK)]
+
+        def shared_copy(dst, src, share):
+            cut = share // 4
+            if cut:
+                nc.vector.tensor_copy(out=dst[:, :cut], in_=src[:, :cut])
+            nc.scalar.activation(out=dst[:, cut:], in_=src[:, cut:], func=COPY)
+
+        for g in range(PASSES):
+            for c0, width, share in X_CHUNKS[g]:
+                grouped = sb([P, width * PACK], BF16, f"x_bf{g}_{c0}")
+                shared_copy(
+                    grouped[:].rearrange("p (c i j) -> p c j i", i=4, j=PACK),
+                    x_raw[g, c0][:].rearrange("p j (c i) -> p c j i", i=4),
+                    share,
+                )
+                nc.vector.quantize_mx(
+                    out=x_words[g][:, c0 : c0 + width].bitcast(FP8X4),
+                    scales=x_scales[g][:, c0 : c0 + width],
+                    in_=grouped[:],
+                )
+            nc.vector.tensor_copy(out=xg_scales[g][:], in_=x_scales[g][:].indirect(offs_sb[:]))
+            nc.vector.tensor_copy(out=xg_words[g][:], in_=x_words[g][:].indirect(offs_sb[:]))
+            for c0, width, share in W_CHUNKS[g]:
+                shared_copy(
+                    w_bf[g][:].rearrange("p (t m j) -> p m j t", t=PACK, j=PACK)[:, c0 // 4 : (c0 + width) // 4],
+                    w_raw[g, c0][:].rearrange("p j (m t) -> p m j t", t=PACK),
+                    share,
+                )
+            step = H if g == 0 else P
+            for c0 in range(0, H, step):
+                nc.vector.quantize_mx(
+                    out=w_words[g][:, c0 : c0 + step].bitcast(FP8X4),
+                    scales=w_scales[g][:, c0 : c0 + step],
+                    in_=w_bf[g][:, c0 * PACK : (c0 + step) * PACK],
+                )
+            for n, (t, s0, width) in enumerate(pieces):
+                cols = slice(t * P, (t + 1) * P)
+                nc.tensor.matmul_mx(
+                    out=h_ps[n][:],
+                    lhsT=w_words[g][:, cols].bitcast(FP8X4),
+                    lhsT_scale=w_scales[g][:, cols],
+                    rhs=xg_words[g][:, s0 : s0 + width].bitcast(FP8X4),
+                    rhs_scale=xg_scales[g][:, s0 : s0 + width],
+                    start=(g == 0),
+                    stop=(g == PASSES - 1),
+                )
+        for n, (t, s0, width) in enumerate(pieces):
+            if n == 1:
+                nc.vector.tensor_scalar_max(out=h[t][:, s0 : s0 + width], in0=h_ps[n][:], scalar1=0.0)
+            else:
+                nc.scalar.activation(out=h[t][:, s0 : s0 + width], in_=h_ps[n][:], func=RELU)
+
+        nb1 = sb([P, PACK, V], BF16, "nb1")
+        nb2 = sb([P, PACK, V], BF16, "nb2")
+        z_planes = sb([P, PACK, V], BF16, "z_planes")
+        c_planes = nb1
+        for t in range(PACK):
+            nc.vector.tensor_copy(out=nb1[:, t, :], in_=h[t][:].indirect(pos1_sb[:]))
+            nc.vector.tensor_copy(out=nb2[:, t, :], in_=h[t][:].indirect(pos2_sb[:]))
+        nc.vector.tensor_tensor(out=z_planes[:], in0=nb1[:], in1=nb2[:], op=MAX)
+        z_bf = sb([P, V * PACK], BF16, "z_bf")
+        nc.scalar.activation(
+            out=z_bf[:].rearrange("p (c i j) -> p c j i", i=4, j=PACK),
+            in_=z_planes[:].rearrange("p j (c i) -> p c j i", i=4),
+            func=COPY,
+        )
+        for t in range(PACK):
+            nc.vector.tensor_copy(out=c_planes[:, t, :], in_=h[t][:].indirect(cen_sb[:]))
+        c_bf = sb([P, V * PACK], BF16, "c_bf")
+        dst = c_bf[:].rearrange("p (c i j) -> p c j i", i=4, j=PACK)
+        src = c_planes[:].rearrange("p j (c i) -> p c j i", i=4)
+        cut = CEN_VECTOR // 4
+        nc.vector.tensor_copy(out=dst[:, :cut], in_=src[:, :cut])
+        nc.scalar.activation(out=dst[:, cut:], in_=src[:, cut:], func=COPY)
+
+        a_words = [sb([P, V], U32, f"a_words{a}") for a in range(2)]
+        a_scales = [sb([P, V], U8, f"a_scales{a}") for a in range(2)]
+        for a, grouped in enumerate((z_bf, c_bf)):
+            nc.vector.quantize_mx(out=a_words[a][:].bitcast(FP8X4), scales=a_scales[a][:], in_=grouped[:])
+
+        o_ps = [psum.tile([P, V], F32, name=f"o_ps{b}") for b in range(N // P)]
+        for a in range(2):
+            for b in range(N // P):
+                cols = slice(b * P, (b + 1) * P)
+                nc.tensor.matmul_mx(
+                    out=o_ps[b][:],
+                    lhsT=w23_words[a][:, cols].bitcast(FP8X4),
+                    lhsT_scale=w23_scales[a][:, cols],
+                    rhs=a_words[a][:].bitcast(FP8X4),
+                    rhs_scale=a_scales[a][:],
+                    start=(a == 0),
+                    stop=(a == 1),
+                )
+        o_sb = [sb([P, V], F32, f"o_sb{b}") for b in range(N // P)]
+        nc.scalar.activation(out=o_sb[0][:], in_=o_ps[0][:], func=COPY)
+        nc.sync.dma_start(out=out[0:P, :], in_=o_sb[0][:])
+        nc.vector.tensor_copy(out=o_sb[1][:], in_=o_ps[1][:])
+        nc.scalar.dma_start(out=out[P : 2 * P, :], in_=o_sb[1][:])

@@ -22,11 +22,10 @@ K_PASS = P * PACK
 PASSES = K // K_PASS
 
 X_CHUNKS = [
-    [(0, 256, 128), (256, 256, 128), (512, 512, 320)],
-    [(0, 256, 0), (256, 256, 0), (512, 256, 0), (768, 128, 0), (896, 128, 80)],
+    [(0, 512, 320), (512, 256, 160), (768, 256, 160)],
+    [(0, 512, 256), (512, 256, 96), (768, 256, 144)],
 ]
-W_CHUNKS = [[(0, 256, 0), (256, 256, 0)], [(0, 192, 0), (192, 192, 0), (384, 128, 0)]]
-CEN_VECTOR = 168
+W_CHUNKS = [[(0, 256, 0), (256, 256, 0)], [(0, 256, 0), (256, 128, 128), (384, 128, 64)]]
 
 
 def tile_picked_sagecat_max_e_kernel(tc, xT, w1, w2_words, w2_scales, w3_words, w3_scales, offs, cen, pos1, pos2, out):
@@ -43,27 +42,29 @@ def tile_picked_sagecat_max_e_kernel(tc, xT, w1, w2_words, w2_scales, w3_words, 
         pos1_sb = sb([P, V // 16], U16, "pos1_sb")
         pos2_sb = sb([P, V // 16], U16, "pos2_sb")
 
-        x_scales = [sb([P, T], U8, f"x_scales{g}") for g in range(PASSES)]
-        for g in range(PASSES):
-            nc.vector.memset(x_scales[g][:].bitcast(I32), 0)
+        x_scales = sb([P, T], U8, "x_scales")
+        nc.vector.memset(x_scales[:].bitcast(I32), 0)
         w23_scales = [sb([P, N], U8, f"w23_scales{a}") for a in range(2)]
         for a in range(2):
             nc.vector.memset(w23_scales[a][:].bitcast(I32), 0)
 
         x_raw, w_raw = {}, {}
-        for g in range(PASSES):
-            for src, chunks, raws, label in ((xT, X_CHUNKS, x_raw, "x"), (w1, W_CHUNKS, w_raw, "w")):
-                rows = src[g * K_PASS : (g + 1) * K_PASS, :].rearrange("(p j) c -> p j c", j=PACK)
-                for c0, width, share in chunks[g]:
-                    raws[g, c0] = sb([P, PACK, width], F32, f"{label}_raw{g}_{c0}")
-                    nc.sync.dma_start(out=raws[g, c0][:], in_=rows[:, :, c0 : c0 + width])
-                if g == 0 and label == "x":
-                    nc.sync.dma_start(offs_sb[:], offs)
+        def load(src, chunks, raws, label, g):
+            rows = src[g * K_PASS : (g + 1) * K_PASS, :].rearrange("(p j) c -> p j c", j=PACK)
+            for c0, width, share in chunks[g]:
+                raws[g, c0] = sb([P, PACK, width], F32, f"{label}_raw{g}_{c0}")
+                nc.sync.dma_start(out=raws[g, c0][:], in_=rows[:, :, c0 : c0 + width])
+
+        load(xT, X_CHUNKS, x_raw, "x", 0)
+        nc.sync.dma_start(offs_sb[:], offs)
+        load(xT, X_CHUNKS, x_raw, "x", 1)
+        load(w1, W_CHUNKS, w_raw, "w", 0)
+        load(w1, W_CHUNKS, w_raw, "w", 1)
+        nc.sync.dma_start(cen_sb[:], cen)
         nc.sync.dma_start(pos1_sb[:], pos1)
         nc.sync.dma_start(pos2_sb[:], pos2)
-        nc.sync.dma_start(cen_sb[:], cen)
         w23_words = [sb([P, N], U32, f"w23_words{a}") for a in range(2)]
-        for a, (words, scales) in enumerate(((w3_words, w3_scales), (w2_words, w2_scales))):
+        for a, (words, scales) in enumerate(((w2_words, w2_scales), (w3_words, w3_scales))):
             nc.sync.dma_start(out=w23_words[a][:].bitcast(I32), in_=words[0].rearrange("p n t -> p (n t)").bitcast(I32))
             for q in range(4):
                 nc.sync.dma_start(
@@ -73,10 +74,12 @@ def tile_picked_sagecat_max_e_kernel(tc, xT, w1, w2_words, w2_scales, w3_words, 
 
         x_words = [sb([P, T], U32, f"x_words{g}") for g in range(PASSES)]
         xg_words = [sb([P, S], U32, f"xg_words{g}") for g in range(PASSES)]
-        xg_scales = [sb([P, S], U8, f"xg_scales{g}") for g in range(PASSES)]
+        xg_scales = sb([P, S], U8, "xg_scales")
         w_bf = [sb([P, H * PACK], BF16, f"w_bf{g}") for g in range(PASSES)]
         w_words = [sb([P, H], U32, f"w_words{g}") for g in range(PASSES)]
-        w_scales = [sb([P, H], U8, f"w_scales{g}") for g in range(PASSES)]
+        shared_planes = sb([P, P], U8, "shared_planes")
+        w_scales = {(g, t): sb([P, P], U8, f"w_scales{g}_{t}")[:] for g, t in ((0, 0), (0, 1), (1, 0), (1, 2), (1, 3))}
+        w_scales.update({(1, 1): shared_planes[:], (0, 2): shared_planes[4:P, :], (0, 3): shared_planes[8:P, :]})
         pieces = [(0, 0, S // 2), (0, S // 2, S // 2)] + [(t, 0, S) for t in range(1, PACK)]
         h_ps = [psum.tile([P, width], F32, name=f"h_ps{n}") for n, (t, s0, width) in enumerate(pieces)]
         h = [sb([P, S], F32, f"h{t}") for t in range(PACK)]
@@ -85,9 +88,10 @@ def tile_picked_sagecat_max_e_kernel(tc, xT, w1, w2_words, w2_scales, w3_words, 
             cut = share // 4
             if cut:
                 nc.vector.tensor_copy(out=dst[:, :cut], in_=src[:, :cut])
-            nc.scalar.activation(out=dst[:, cut:], in_=src[:, cut:], func=COPY)
+            if cut < dst.shape[1]:
+                nc.scalar.activation(out=dst[:, cut:], in_=src[:, cut:], func=COPY)
 
-        for g in range(PASSES):
+        def prepare_x(g):
             for c0, width, share in X_CHUNKS[g]:
                 grouped = sb([P, width * PACK], BF16, f"x_bf{g}_{c0}")
                 shared_copy(
@@ -97,67 +101,80 @@ def tile_picked_sagecat_max_e_kernel(tc, xT, w1, w2_words, w2_scales, w3_words, 
                 )
                 nc.vector.quantize_mx(
                     out=x_words[g][:, c0 : c0 + width].bitcast(FP8X4),
-                    scales=x_scales[g][:, c0 : c0 + width],
+                    scales=x_scales[4 * g : P, c0 : c0 + width],
                     in_=grouped[:],
                 )
-            nc.vector.tensor_copy(out=xg_scales[g][:], in_=x_scales[g][:].indirect(offs_sb[:]))
-            nc.vector.tensor_copy(out=xg_words[g][:], in_=x_words[g][:].indirect(offs_sb[:]))
+
+        def prepare_w(g):
             for c0, width, share in W_CHUNKS[g]:
                 shared_copy(
                     w_bf[g][:].rearrange("p (t m j) -> p m j t", t=PACK, j=PACK)[:, c0 // 4 : (c0 + width) // 4],
                     w_raw[g, c0][:].rearrange("p j (m t) -> p m j t", t=PACK),
                     share,
                 )
-            step = H if g == 0 else P
-            for c0 in range(0, H, step):
-                nc.vector.quantize_mx(
-                    out=w_words[g][:, c0 : c0 + step].bitcast(FP8X4),
-                    scales=w_scales[g][:, c0 : c0 + step],
-                    in_=w_bf[g][:, c0 * PACK : (c0 + step) * PACK],
-                )
-            for n, (t, s0, width) in enumerate(pieces):
-                cols = slice(t * P, (t + 1) * P)
-                nc.tensor.matmul_mx(
-                    out=h_ps[n][:],
-                    lhsT=w_words[g][:, cols].bitcast(FP8X4),
-                    lhsT_scale=w_scales[g][:, cols],
-                    rhs=xg_words[g][:, s0 : s0 + width].bitcast(FP8X4),
-                    rhs_scale=xg_scales[g][:, s0 : s0 + width],
-                    start=(g == 0),
-                    stop=(g == PASSES - 1),
-                )
+
+        def quantize_w(g, t):
+            nc.vector.quantize_mx(
+                out=w_words[g][:, t * P : (t + 1) * P].bitcast(FP8X4),
+                scales=w_scales[g, t],
+                in_=w_bf[g][:, t * K_PASS : (t + 1) * K_PASS],
+            )
+
+        def first_product(g, n):
+            t, s0, width = pieces[n]
+            nc.tensor.matmul_mx(
+                out=h_ps[n][:],
+                lhsT=w_words[g][:, t * P : (t + 1) * P].bitcast(FP8X4),
+                lhsT_scale=w_scales[g, t],
+                rhs=xg_words[g][:, s0 : s0 + width].bitcast(FP8X4),
+                rhs_scale=xg_scales[4 * g : P, s0 : s0 + width],
+                start=(g == 0),
+                stop=(g == PASSES - 1),
+            )
+
+        prepare_x(0)
+        nc.vector.tensor_copy(out=xg_words[0][:], in_=x_words[0][:].indirect(offs_sb[:]))
+        prepare_x(1)
+        nc.vector.tensor_copy(out=xg_scales[:], in_=x_scales[:].indirect(offs_sb[:]))
+        nc.vector.tensor_copy(out=xg_words[1][:], in_=x_words[1][:].indirect(offs_sb[:]))
+        prepare_w(0)
+        quantize_w(0, 0)
+        quantize_w(0, 1)
+        for n in range(3):
+            first_product(0, n)
+        prepare_w(1)
+        for g, t in ((1, 0), (1, 1), (0, 2), (0, 3), (1, 2), (1, 3)):
+            quantize_w(g, t)
+        for n in range(3):
+            first_product(1, n)
+        for n in range(3, 5):
+            first_product(0, n)
+            first_product(1, n)
         for n, (t, s0, width) in enumerate(pieces):
             if n == 1:
                 nc.vector.tensor_scalar_max(out=h[t][:, s0 : s0 + width], in0=h_ps[n][:], scalar1=0.0)
             else:
                 nc.scalar.activation(out=h[t][:, s0 : s0 + width], in_=h_ps[n][:], func=RELU)
 
-        nb1 = sb([P, PACK, V], BF16, "nb1")
-        nb2 = sb([P, PACK, V], BF16, "nb2")
-        z_planes = sb([P, PACK, V], BF16, "z_planes")
-        c_planes = nb1
+        own, nb1, nb2 = (sb([P, PACK, V], F32, name) for name in ("own", "nb1", "nb2"))
         for t in range(PACK):
-            nc.vector.tensor_copy(out=nb1[:, t, :], in_=h[t][:].indirect(pos1_sb[:]))
-            nc.vector.tensor_copy(out=nb2[:, t, :], in_=h[t][:].indirect(pos2_sb[:]))
-        nc.vector.tensor_tensor(out=z_planes[:], in0=nb1[:], in1=nb2[:], op=MAX)
-        z_bf = sb([P, V * PACK], BF16, "z_bf")
-        nc.scalar.activation(
-            out=z_bf[:].rearrange("p (c i j) -> p c j i", i=4, j=PACK),
-            in_=z_planes[:].rearrange("p j (c i) -> p c j i", i=4),
-            func=COPY,
-        )
-        for t in range(PACK):
-            nc.vector.tensor_copy(out=c_planes[:, t, :], in_=h[t][:].indirect(cen_sb[:]))
+            for planes, offsets in ((own, cen_sb), (nb1, pos1_sb), (nb2, pos2_sb)):
+                nc.vector.tensor_copy(out=planes[:, t, :], in_=h[t][:].indirect(offsets[:]))
         c_bf = sb([P, V * PACK], BF16, "c_bf")
-        dst = c_bf[:].rearrange("p (c i j) -> p c j i", i=4, j=PACK)
-        src = c_planes[:].rearrange("p j (c i) -> p c j i", i=4)
-        cut = CEN_VECTOR // 4
-        nc.vector.tensor_copy(out=dst[:, :cut], in_=src[:, :cut])
-        nc.scalar.activation(out=dst[:, cut:], in_=src[:, cut:], func=COPY)
+        z_bf = sb([P, V * PACK], BF16, "z_bf")
+
+        def planes_view(planes):
+            return planes[:].rearrange("p j (c i) -> p c j i", i=4)
+
+        def grouped_view(grouped):
+            return grouped[:].rearrange("p (c i j) -> p c j i", i=4, j=PACK)
+
+        nc.scalar.activation(out=grouped_view(c_bf), in_=planes_view(own), func=COPY)
+        nc.vector.tensor_tensor(out=grouped_view(z_bf), in0=planes_view(nb1), in1=planes_view(nb2), op=MAX)
 
         a_words = [sb([P, V], U32, f"a_words{a}") for a in range(2)]
         a_scales = [sb([P, V], U8, f"a_scales{a}") for a in range(2)]
-        for a, grouped in enumerate((z_bf, c_bf)):
+        for a, grouped in enumerate((c_bf, z_bf)):
             nc.vector.quantize_mx(out=a_words[a][:].bitcast(FP8X4), scales=a_scales[a][:], in_=grouped[:])
 
         o_ps = [psum.tile([P, V], F32, name=f"o_ps{b}") for b in range(N // P)]

@@ -23,9 +23,10 @@ PASSES = K // K_PASS
 
 X_CHUNKS = [
     [(0, 512, 320), (512, 256, 160), (768, 256, 160)],
-    [(0, 512, 256), (512, 256, 96), (768, 256, 144)],
+    [(0, 256, 0), (256, 256, 48), (512, 256, 64), (768, 128, 128), (896, 128, 80)],
 ]
-W_CHUNKS = [[(0, 256, 0), (256, 256, 0)], [(0, 256, 0), (256, 128, 128), (384, 128, 64)]]
+X_QUANT = [[(0, 512), (512, 256), (768, 256)], [(0, 256), (256, 256), (512, 256), (768, 256)]]
+W_CHUNKS = [[(0, 256, 0), (256, 256, 0)], [(0, 256, 0), (256, 128, 128), (384, 128, 128)]]
 
 
 def tile_picked_sagecat_max_e_kernel(tc, xT, w1, w2_words, w2_scales, w3_words, w3_scales, offs, cen, pos1, pos2, out):
@@ -75,11 +76,11 @@ def tile_picked_sagecat_max_e_kernel(tc, xT, w1, w2_words, w2_scales, w3_words, 
         x_words = [sb([P, T], U32, f"x_words{g}") for g in range(PASSES)]
         xg_words = [sb([P, S], U32, f"xg_words{g}") for g in range(PASSES)]
         xg_scales = sb([P, S], U8, "xg_scales")
-        w_bf = [sb([P, H * PACK], BF16, f"w_bf{g}") for g in range(PASSES)]
-        w_words = [sb([P, H], U32, f"w_words{g}") for g in range(PASSES)]
-        shared_planes = sb([P, P], U8, "shared_planes")
-        w_scales = {(g, t): sb([P, P], U8, f"w_scales{g}_{t}")[:] for g, t in ((0, 0), (0, 1), (1, 0), (1, 2), (1, 3))}
-        w_scales.update({(1, 1): shared_planes[:], (0, 2): shared_planes[4:P, :], (0, 3): shared_planes[8:P, :]})
+        slots = [(g, t) for t in range(PACK) for g in range(PASSES)]
+        w_lo = sb([P, 4 * K_PASS], BF16, "w_lo")
+        w_hi = sb([P, 4 * K_PASS], BF16, "w_hi")
+        w_words = sb([P, len(slots) * P], U32, "w_words")
+        w_scales = sb([P, len(slots) * P], U8, "w_scales")
         pieces = [(0, 0, S // 2), (0, S // 2, S // 2)] + [(t, 0, S) for t in range(1, PACK)]
         h_ps = [psum.tile([P, width], F32, name=f"h_ps{n}") for n, (t, s0, width) in enumerate(pieces)]
         h = [sb([P, S], F32, f"h{t}") for t in range(PACK)]
@@ -92,40 +93,41 @@ def tile_picked_sagecat_max_e_kernel(tc, xT, w1, w2_words, w2_scales, w3_words, 
                 nc.scalar.activation(out=dst[:, cut:], in_=src[:, cut:], func=COPY)
 
         def prepare_x(g):
-            for c0, width, share in X_CHUNKS[g]:
-                grouped = sb([P, width * PACK], BF16, f"x_bf{g}_{c0}")
-                shared_copy(
-                    grouped[:].rearrange("p (c i j) -> p c j i", i=4, j=PACK),
-                    x_raw[g, c0][:].rearrange("p j (c i) -> p c j i", i=4),
-                    share,
-                )
+            for q0, q_width in X_QUANT[g]:
+                grouped = sb([P, q_width * PACK], BF16, f"x_bf{g}_{q0}")
+                for c0, width, share in X_CHUNKS[g]:
+                    if q0 <= c0 < q0 + q_width:
+                        shared_copy(
+                            grouped[:, (c0 - q0) * PACK : (c0 - q0 + width) * PACK].rearrange("p (c i j) -> p c j i", i=4, j=PACK),
+                            x_raw[g, c0][:].rearrange("p j (c i) -> p c j i", i=4),
+                            share,
+                        )
                 nc.vector.quantize_mx(
-                    out=x_words[g][:, c0 : c0 + width].bitcast(FP8X4),
-                    scales=x_scales[4 * g : P, c0 : c0 + width],
+                    out=x_words[g][:, q0 : q0 + q_width].bitcast(FP8X4),
+                    scales=x_scales[4 * g : P, q0 : q0 + q_width],
                     in_=grouped[:],
                 )
 
-        def prepare_w(g):
+        def round_w(g, upper):
+            dealt = (w_hi if upper else w_lo)[:].rearrange("p (t g m j) -> p g m j t", t=2, g=PASSES, j=PACK)[:, g]
             for c0, width, share in W_CHUNKS[g]:
                 shared_copy(
-                    w_bf[g][:].rearrange("p (t m j) -> p m j t", t=PACK, j=PACK)[:, c0 // 4 : (c0 + width) // 4],
-                    w_raw[g, c0][:].rearrange("p j (m t) -> p m j t", t=PACK),
-                    share,
+                    dealt[:, c0 // 4 : (c0 + width) // 4],
+                    w_raw[g, c0][:].rearrange("p j (m t) -> p m j t", t=PACK)[:, :, :, 2 * upper : 2 * upper + 2],
+                    0 if upper else share,
                 )
 
-        def quantize_w(g, t):
-            nc.vector.quantize_mx(
-                out=w_words[g][:, t * P : (t + 1) * P].bitcast(FP8X4),
-                scales=w_scales[g, t],
-                in_=w_bf[g][:, t * K_PASS : (t + 1) * K_PASS],
-            )
+        def quantize_w(first, source):
+            cols = slice(first * P, first * P + source.shape[1] // PACK)
+            nc.vector.quantize_mx(out=w_words[:, cols].bitcast(FP8X4), scales=w_scales[:, cols], in_=source)
 
         def first_product(g, n):
             t, s0, width = pieces[n]
+            slot = slots.index((g, t))
             nc.tensor.matmul_mx(
                 out=h_ps[n][:],
-                lhsT=w_words[g][:, t * P : (t + 1) * P].bitcast(FP8X4),
-                lhsT_scale=w_scales[g, t],
+                lhsT=w_words[:, slot * P : (slot + 1) * P].bitcast(FP8X4),
+                lhsT_scale=w_scales[:, slot * P : (slot + 1) * P],
                 rhs=xg_words[g][:, s0 : s0 + width].bitcast(FP8X4),
                 rhs_scale=xg_scales[4 * g : P, s0 : s0 + width],
                 start=(g == 0),
@@ -137,24 +139,32 @@ def tile_picked_sagecat_max_e_kernel(tc, xT, w1, w2_words, w2_scales, w3_words, 
         prepare_x(1)
         nc.vector.tensor_copy(out=xg_scales[:], in_=x_scales[:].indirect(offs_sb[:]))
         nc.vector.tensor_copy(out=xg_words[1][:], in_=x_words[1][:].indirect(offs_sb[:]))
-        prepare_w(0)
-        quantize_w(0, 0)
-        quantize_w(0, 1)
-        for n in range(3):
-            first_product(0, n)
-        prepare_w(1)
-        for g, t in ((1, 0), (1, 1), (0, 2), (0, 3), (1, 2), (1, 3)):
-            quantize_w(g, t)
-        for n in range(3):
-            first_product(1, n)
-        for n in range(3, 5):
-            first_product(0, n)
-            first_product(1, n)
-        for n, (t, s0, width) in enumerate(pieces):
+        round_w(0, 0)
+        quantize_w(0, w_lo[:, :K_PASS])
+        round_w(1, 0)
+        quantize_w(1, w_lo[:, K_PASS : 2 * K_PASS])
+        quantize_w(2, w_lo[:, 2 * K_PASS :])
+        def relu(n):
+            t, s0, width = pieces[n]
             if n == 1:
                 nc.vector.tensor_scalar_max(out=h[t][:, s0 : s0 + width], in0=h_ps[n][:], scalar1=0.0)
             else:
                 nc.scalar.activation(out=h[t][:, s0 : s0 + width], in_=h_ps[n][:], func=RELU)
+
+        for g in range(PASSES):
+            first_product(g, 0)
+            first_product(g, 1)
+        for g in range(PASSES):
+            first_product(g, 2)
+        for n in range(3):
+            relu(n)
+        for g in range(PASSES):
+            round_w(g, 1)
+        quantize_w(4, w_hi[:])
+        for n in range(3, 5):
+            first_product(0, n)
+            first_product(1, n)
+            relu(n)
 
         own, nb1, nb2 = (sb([P, PACK, V], F32, name) for name in ("own", "nb1", "nb2"))
         for t in range(PACK):

@@ -85,8 +85,7 @@ def tile_picked_sagecat_max_e_kernel(tc, xT, w1, w2_words, w2_scales, w3_words, 
         h_ps = [psum.tile([P, width], F32, name=f"h_ps{n}") for n, (t, s0, width) in enumerate(pieces)]
         h = [sb([P, S], F32, f"h{t}") for t in range(PACK)]
 
-        def shared_copy(dst, src, share):
-            cut = share // 4
+        def shared_copy(dst, src, cut):
             if cut:
                 nc.vector.tensor_copy(out=dst[:, :cut], in_=src[:, :cut])
             if cut < dst.shape[1]:
@@ -98,9 +97,9 @@ def tile_picked_sagecat_max_e_kernel(tc, xT, w1, w2_words, w2_scales, w3_words, 
                 for c0, width, share in X_CHUNKS[g]:
                     if q0 <= c0 < q0 + q_width:
                         shared_copy(
-                            grouped[:, (c0 - q0) * PACK : (c0 - q0 + width) * PACK].rearrange("p (c i j) -> p c j i", i=4, j=PACK),
-                            x_raw[g, c0][:].rearrange("p j (c i) -> p c j i", i=4),
-                            share,
+                            grouped[:, (c0 - q0) * PACK : (c0 - q0 + width) * PACK].rearrange("p (c i j) -> p c j i", i=2, j=PACK),
+                            x_raw[g, c0][:].rearrange("p j (c i) -> p c j i", i=2),
+                            share // 2,
                         )
                 nc.vector.quantize_mx(
                     out=x_words[g][:, q0 : q0 + q_width].bitcast(FP8X4),
@@ -114,7 +113,7 @@ def tile_picked_sagecat_max_e_kernel(tc, xT, w1, w2_words, w2_scales, w3_words, 
                 shared_copy(
                     dealt[:, c0 // 4 : (c0 + width) // 4],
                     w_raw[g, c0][:].rearrange("p j (m t) -> p m j t", t=PACK)[:, :, :, 2 * upper : 2 * upper + 2],
-                    0 if upper else share,
+                    0 if upper else share // 4,
                 )
 
         def quantize_w(first, source):
@@ -174,10 +173,10 @@ def tile_picked_sagecat_max_e_kernel(tc, xT, w1, w2_words, w2_scales, w3_words, 
         z_bf = sb([P, V * PACK], BF16, "z_bf")
 
         def planes_view(planes):
-            return planes[:].rearrange("p j (c i) -> p c j i", i=4)
+            return planes[:].rearrange("p j (c i) -> p c j i", i=2)
 
         def grouped_view(grouped):
-            return grouped[:].rearrange("p (c i j) -> p c j i", i=4, j=PACK)
+            return grouped[:].rearrange("p (c i j) -> p c j i", i=2, j=PACK)
 
         nc.scalar.activation(out=grouped_view(c_bf), in_=planes_view(own), func=COPY)
         nc.vector.tensor_tensor(out=grouped_view(z_bf), in0=planes_view(nb1), in1=planes_view(nb2), op=MAX)

@@ -23,7 +23,7 @@ PASSES = K // K_PASS
 
 X_CHUNKS = [
     [(0, 512, 320), (512, 256, 160), (768, 256, 160)],
-    [(0, 256, 0), (256, 256, 48), (512, 256, 64), (768, 128, 128), (896, 128, 80)],
+    [(0, 256, 0), (256, 256, 48), (512, 256, 64), (768, 256, 160)],
 ]
 X_QUANT = [[(0, 512), (512, 256), (768, 256)], [(0, 256), (256, 256), (512, 256), (768, 256)]]
 W_CHUNKS = [[(0, 256, 0), (256, 256, 0)], [(0, 256, 0), (256, 128, 128), (384, 128, 128)]]
@@ -35,8 +35,8 @@ def tile_picked_sagecat_max_e_kernel(tc, xT, w1, w2_words, w2_scales, w3_words, 
         keep = ctx.enter_context(tc.tile_pool(name="keep", bufs=1))
         psum = ctx.enter_context(tc.psum_pool(name="psum", bufs=1))
 
-        def sb(shape, dtype, name):
-            return keep.tile(shape, dtype, name=name, align_bytes=64)
+        def sb(shape, dtype, name, tag=None):
+            return keep.tile(shape, dtype, name=name, tag=tag or name, align_bytes=64)
 
         offs_sb = sb([P, S // 16], U16, "offs_sb")
         cen_sb = sb([P, V // 16], U16, "cen_sb")
@@ -76,13 +76,14 @@ def tile_picked_sagecat_max_e_kernel(tc, xT, w1, w2_words, w2_scales, w3_words, 
         x_words = [sb([P, T], U32, f"x_words{g}") for g in range(PASSES)]
         xg_words = [sb([P, S], U32, f"xg_words{g}") for g in range(PASSES)]
         xg_scales = sb([P, S], U8, "xg_scales")
-        slots = [(g, t) for t in range(PACK) for g in range(PASSES)]
-        w_lo = sb([P, 4 * K_PASS], BF16, "w_lo")
-        w_hi = sb([P, 4 * K_PASS], BF16, "w_hi")
-        w_words = sb([P, len(slots) * P], U32, "w_words")
-        w_scales = sb([P, len(slots) * P], U8, "w_scales")
-        pieces = [(0, 0, S // 2), (0, S // 2, S // 2)] + [(t, 0, S) for t in range(1, PACK)]
-        h_ps = [psum.tile([P, width], F32, name=f"h_ps{n}") for n, (t, s0, width) in enumerate(pieces)]
+        w_bf0 = sb([P, 4 * K_PASS], BF16, "w_bf0")
+        w_lo = sb([P, 2 * K_PASS], BF16, "w_lo")
+        w_hi = sb([P, 2 * K_PASS], BF16, "w_hi")
+        w_words = [sb([P, H], U32, f"w_words{g}") for g in range(PASSES)]
+        w_planes = sb([P, H + 2 * P], U8, "w_planes")
+        w_scales = {(g, t): w_planes[4 * g : P, (t + 2 * g) * P : (t + 2 * g + 1) * P] for g in range(PASSES) for t in range(PACK)}
+        pieces = [(0, 0, 2 * P), (0, 2 * P, P), (0, 3 * P, P)] + [(t, 0, S) for t in range(1, PACK)]
+        h_ps = [psum.tile([P, width], F32, name=f"h_ps{n}", tag=f"h_ps{n}") for n, (t, s0, width) in enumerate(pieces)]
         h = [sb([P, S], F32, f"h{t}") for t in range(PACK)]
 
         def shared_copy(dst, src, cut):
@@ -107,26 +108,21 @@ def tile_picked_sagecat_max_e_kernel(tc, xT, w1, w2_words, w2_scales, w3_words, 
                     in_=grouped[:],
                 )
 
-        def round_w(g, upper):
-            dealt = (w_hi if upper else w_lo)[:].rearrange("p (t g m j) -> p g m j t", t=2, g=PASSES, j=PACK)[:, g]
+        def round_w(g, dst, t0, tiles):
+            dealt = dst[:].rearrange("p (t m j) -> p m j t", t=tiles, j=PACK)
             for c0, width, share in W_CHUNKS[g]:
                 shared_copy(
                     dealt[:, c0 // 4 : (c0 + width) // 4],
-                    w_raw[g, c0][:].rearrange("p j (m t) -> p m j t", t=PACK)[:, :, :, 2 * upper : 2 * upper + 2],
-                    0 if upper else share // 4,
+                    w_raw[g, c0][:].rearrange("p j (m t) -> p m j t", t=PACK)[:, :, :, t0 : t0 + tiles],
+                    0 if t0 else share // 4,
                 )
-
-        def quantize_w(first, source):
-            cols = slice(first * P, first * P + source.shape[1] // PACK)
-            nc.vector.quantize_mx(out=w_words[:, cols].bitcast(FP8X4), scales=w_scales[:, cols], in_=source)
 
         def first_product(g, n):
             t, s0, width = pieces[n]
-            slot = slots.index((g, t))
             nc.tensor.matmul_mx(
                 out=h_ps[n][:],
-                lhsT=w_words[:, slot * P : (slot + 1) * P].bitcast(FP8X4),
-                lhsT_scale=w_scales[:, slot * P : (slot + 1) * P],
+                lhsT=w_words[g][:, t * P : (t + 1) * P].bitcast(FP8X4),
+                lhsT_scale=w_scales[g, t],
                 rhs=xg_words[g][:, s0 : s0 + width].bitcast(FP8X4),
                 rhs_scale=xg_scales[4 * g : P, s0 : s0 + width],
                 start=(g == 0),
@@ -138,29 +134,34 @@ def tile_picked_sagecat_max_e_kernel(tc, xT, w1, w2_words, w2_scales, w3_words, 
         prepare_x(1)
         nc.vector.tensor_copy(out=xg_scales[:], in_=x_scales[:].indirect(offs_sb[:]))
         nc.vector.tensor_copy(out=xg_words[1][:], in_=x_words[1][:].indirect(offs_sb[:]))
-        round_w(0, 0)
-        quantize_w(0, w_lo[:, :K_PASS])
-        round_w(1, 0)
-        quantize_w(1, w_lo[:, K_PASS : 2 * K_PASS])
-        quantize_w(2, w_lo[:, 2 * K_PASS :])
+        round_w(0, w_bf0, 0, PACK)
+        for t in (0, 2):
+            nc.vector.quantize_mx(
+                out=w_words[0][:, t * P : (t + 2) * P].bitcast(FP8X4),
+                scales=w_planes[:, t * P : (t + 2) * P],
+                in_=w_bf0[:, t * K_PASS : (t + 2) * K_PASS],
+            )
+        round_w(1, w_lo, 0, 2)
+        for t in range(2):
+            nc.vector.quantize_mx(
+                out=w_words[1][:, t * P : (t + 1) * P].bitcast(FP8X4), scales=w_scales[1, t], in_=w_lo[:, t * K_PASS : (t + 1) * K_PASS]
+            )
+
         def relu(n):
             t, s0, width = pieces[n]
-            if n == 1:
+            if s0:
                 nc.vector.tensor_scalar_max(out=h[t][:, s0 : s0 + width], in0=h_ps[n][:], scalar1=0.0)
             else:
                 nc.scalar.activation(out=h[t][:, s0 : s0 + width], in_=h_ps[n][:], func=RELU)
 
         for g in range(PASSES):
-            first_product(g, 0)
-            first_product(g, 1)
-        for g in range(PASSES):
-            first_product(g, 2)
-        for n in range(3):
+            for n in range(4):
+                first_product(g, n)
+        for n in range(4):
             relu(n)
-        for g in range(PASSES):
-            round_w(g, 1)
-        quantize_w(4, w_hi[:])
-        for n in range(3, 5):
+        round_w(1, w_hi, 2, 2)
+        nc.vector.quantize_mx(out=w_words[1][:, 2 * P :].bitcast(FP8X4), scales=w_planes[4:P, H:], in_=w_hi[:])
+        for n in range(4, 6):
             first_product(0, n)
             first_product(1, n)
             relu(n)
@@ -168,39 +169,56 @@ def tile_picked_sagecat_max_e_kernel(tc, xT, w1, w2_words, w2_scales, w3_words, 
         own, nb1, nb2 = (sb([P, PACK, V], F32, name) for name in ("own", "nb1", "nb2"))
         for t in range(PACK):
             for planes, offsets in ((own, cen_sb), (nb1, pos1_sb), (nb2, pos2_sb)):
-                nc.vector.tensor_copy(out=planes[:, t, :], in_=h[t][:].indirect(offsets[:]))
-        c_bf = sb([P, V * PACK], BF16, "c_bf")
-        z_bf = sb([P, V * PACK], BF16, "z_bf")
+                cuts = (0, P, V) if (t == PACK - 1 and offsets is pos2_sb) else (0, V)
+                for v0, v1 in zip(cuts, cuts[1:]):
+                    nc.vector.tensor_copy(out=planes[:, t, v0:v1], in_=h[t][:].indirect(offsets[:, v0 // 16 : v1 // 16]))
 
-        def planes_view(planes):
-            return planes[:].rearrange("p j (c i) -> p c j i", i=2)
+        def planes_view(planes, u):
+            return planes[:, :, u * P : (u + 1) * P].rearrange("p j (c i) -> p c j i", i=4)
 
         def grouped_view(grouped):
-            return grouped[:].rearrange("p (c i j) -> p c j i", i=2, j=PACK)
+            return grouped[:].rearrange("p (c i j) -> p c j i", i=4, j=PACK)
 
-        nc.scalar.activation(out=grouped_view(c_bf), in_=planes_view(own), func=COPY)
-        nc.vector.tensor_tensor(out=grouped_view(z_bf), in0=planes_view(nb1), in1=planes_view(nb2), op=MAX)
+        c_bf = [sb([P, K_PASS], BF16, f"c_bf{u}") for u in range(2)]
+        z_bf = [sb([P, K_PASS], BF16, f"z_bf{u}") for u in range(2)]
+        a_words = {(a, u): sb([P, P], U32, f"a_words{a}_{u}") for a in range(2) for u in range(2)}
+        a_scales = {(a, u): sb([P, P], U8, f"a_scales{a}_{u}") for a in range(2) for u in range(2)}
 
-        a_words = [sb([P, V], U32, f"a_words{a}") for a in range(2)]
-        a_scales = [sb([P, V], U8, f"a_scales{a}") for a in range(2)]
-        for a, grouped in enumerate((c_bf, z_bf)):
-            nc.vector.quantize_mx(out=a_words[a][:].bitcast(FP8X4), scales=a_scales[a][:], in_=grouped[:])
+        def quantize(a, u):
+            nc.vector.quantize_mx(out=a_words[a, u][:].bitcast(FP8X4), scales=a_scales[a, u][:], in_=(c_bf, z_bf)[a][u][:])
 
-        o_ps = [psum.tile([P, V], F32, name=f"o_ps{b}") for b in range(N // P)]
-        for a in range(2):
-            for b in range(N // P):
-                cols = slice(b * P, (b + 1) * P)
-                nc.tensor.matmul_mx(
-                    out=o_ps[b][:],
-                    lhsT=w23_words[a][:, cols].bitcast(FP8X4),
-                    lhsT_scale=w23_scales[a][:, cols],
-                    rhs=a_words[a][:].bitcast(FP8X4),
-                    rhs_scale=a_scales[a][:],
-                    start=(a == 0),
-                    stop=(a == 1),
-                )
-        o_sb = [sb([P, V], F32, f"o_sb{b}") for b in range(N // P)]
-        nc.scalar.activation(out=o_sb[0][:], in_=o_ps[0][:], func=COPY)
-        nc.sync.dma_start(out=out[0:P, :], in_=o_sb[0][:])
-        nc.vector.tensor_copy(out=o_sb[1][:], in_=o_ps[1][:])
-        nc.scalar.dma_start(out=out[P : 2 * P, :], in_=o_sb[1][:])
+        def largest(u):
+            nc.vector.tensor_tensor(out=grouped_view(z_bf[u]), in0=planes_view(nb1, u), in1=planes_view(nb2, u), op=MAX)
+
+        for u in range(2):
+            nc.scalar.activation(out=grouped_view(c_bf[u]), in_=planes_view(own, u), func=COPY)
+        largest(0)
+        quantize(0, 0)
+        largest(1)
+        quantize(1, 0)
+        quantize(0, 1)
+        quantize(1, 1)
+
+        o_ps = {(u, b): psum.tile([P, P], F32, name=f"o_ps{u}_{b}", tag=f"h_ps{2 * u + b}") for u in range(2) for b in range(N // P)}
+        for u in range(2):
+            for a in range(2):
+                for b in range(N // P):
+                    cols = slice(b * P, (b + 1) * P)
+                    nc.tensor.matmul_mx(
+                        out=o_ps[u, b][:],
+                        lhsT=w23_words[a][:, cols].bitcast(FP8X4),
+                        lhsT_scale=w23_scales[a][:, cols],
+                        rhs=a_words[a, u][:].bitcast(FP8X4),
+                        rhs_scale=a_scales[a, u][:],
+                        start=(a == 0),
+                        stop=(a == 1),
+                    )
+        o_first = sb([P, N // P, P], F32, "o_first")
+        for b in range(N // P):
+            nc.scalar.activation(out=o_first[:, b, :], in_=o_ps[0, b][:], func=COPY)
+        nc.sync.dma_start(out=out[:, :P].rearrange("(b p) v -> p b v", p=P), in_=o_first[:])
+        o_sb = [sb([P, P], F32, f"o_sb{b}") for b in range(N // P)]
+        nc.scalar.activation(out=o_sb[0][:], in_=o_ps[1, 0][:], func=COPY)
+        nc.sync.dma_start(out=out[0:P, P:], in_=o_sb[0][:])
+        nc.vector.tensor_copy(out=o_sb[1][:], in_=o_ps[1, 1][:])
+        nc.scalar.dma_start(out=out[P : 2 * P, P:], in_=o_sb[1][:])

@@ -20,13 +20,14 @@ P = 128
 PACK = 4
 K_PASS = P * PACK
 PASSES = K // K_PASS
+HALF = H // 2
 
-X_CHUNKS = [
-    [(0, 512, 320), (512, 256, 160), (768, 256, 160)],
-    [(0, 256, 0), (256, 256, 48), (512, 256, 64), (768, 256, 160)],
-]
-X_QUANT = [[(0, 512), (512, 256), (768, 256)], [(0, 256), (256, 256), (512, 256), (768, 256)]]
-W_CHUNKS = [[(0, 256, 0), (256, 256, 0)], [(0, 256, 0), (256, 128, 128), (384, 128, 128)]]
+X_CHUNKS = {
+    (0, 0): [(0, 512, 256), (512, 512, 320)],
+    (0, 1): [(0, 512, 0), (512, 512, 320)],
+    (1, 0): [(0, 512, 0), (512, 512, 192)],
+    (1, 1): [(0, 512, 0), (512, 384, 256), (896, 128, 0)],
+}
 
 
 def tile_picked_sagecat_max_e_kernel(tc, xT, w1, w2_words, w2_scales, w3_words, w3_scales, offs, cen, pos1, pos2, out):
@@ -43,27 +44,30 @@ def tile_picked_sagecat_max_e_kernel(tc, xT, w1, w2_words, w2_scales, w3_words, 
         pos1_sb = sb([P, V // 16], U16, "pos1_sb")
         pos2_sb = sb([P, V // 16], U16, "pos2_sb")
 
-        x_scales = sb([P, T], U8, "x_scales")
-        nc.vector.memset(x_scales[:].bitcast(I32), 0)
         w23_scales = [sb([P, N], U8, f"w23_scales{a}") for a in range(2)]
         for a in range(2):
             nc.vector.memset(w23_scales[a][:].bitcast(I32), 0)
 
-        x_raw, w_raw = {}, {}
-        def load(src, chunks, raws, label, g):
-            rows = src[g * K_PASS : (g + 1) * K_PASS, :].rearrange("(p j) c -> p j c", j=PACK)
-            for c0, width, share in chunks[g]:
-                raws[g, c0] = sb([P, PACK, width], F32, f"{label}_raw{g}_{c0}")
-                nc.sync.dma_start(out=raws[g, c0][:], in_=rows[:, :, c0 : c0 + width])
+        x_raw, w_raw, x_bf = {}, {}, {}
 
-        load(xT, X_CHUNKS, x_raw, "x", 0)
-        nc.sync.dma_start(offs_sb[:], offs)
-        load(xT, X_CHUNKS, x_raw, "x", 1)
-        load(w1, W_CHUNKS, w_raw, "w", 0)
-        load(w1, W_CHUNKS, w_raw, "w", 1)
-        nc.sync.dma_start(cen_sb[:], cen)
-        nc.sync.dma_start(pos1_sb[:], pos1)
-        nc.sync.dma_start(pos2_sb[:], pos2)
+        def load(src, g, j0, rows, c0, width, name):
+            view = src[g * K_PASS : (g + 1) * K_PASS, :].rearrange("(p j) c -> p j c", j=PACK)
+            raw = sb([P, rows, width], F32, name)
+            nc.sync.dma_start(out=raw[:], in_=view[:, j0 : j0 + rows, c0 : c0 + width])
+            return raw
+
+        for (g, u), chunks in X_CHUNKS.items():
+            for c0, width, share in chunks:
+                x_raw[g, u, c0] = load(xT, g, 2 * u, 2, c0, width, f"x_raw{g}_{u}_{c0}")
+            if (g, u) == (0, 0):
+                nc.sync.dma_start(offs_sb[:], offs)
+        for half in range(2):
+            for g in range(PASSES):
+                w_raw[half, g] = load(w1, g, 0, PACK, half * HALF, HALF, f"w_raw{half}_{g}")
+            if half == 0:
+                nc.sync.dma_start(pos1_sb[:], pos1)
+                nc.sync.dma_start(pos2_sb[:], pos2)
+                nc.sync.dma_start(cen_sb[:], cen)
         w23_words = [sb([P, N], U32, f"w23_words{a}") for a in range(2)]
         for a, (words, scales) in enumerate(((w2_words, w2_scales), (w3_words, w3_scales))):
             nc.sync.dma_start(out=w23_words[a][:].bitcast(I32), in_=words[0].rearrange("p n t -> p (n t)").bitcast(I32))
@@ -73,108 +77,151 @@ def tile_picked_sagecat_max_e_kernel(tc, xT, w1, w2_words, w2_scales, w3_words, 
                     in_=scales[0, 4 * q : 4 * q + 4, :].bitcast(I32),
                 )
 
-        x_words = [sb([P, T], U32, f"x_words{g}") for g in range(PASSES)]
-        xg_words = [sb([P, S], U32, f"xg_words{g}") for g in range(PASSES)]
-        xg_scales = sb([P, S], U8, "xg_scales")
-        w_bf0 = sb([P, 4 * K_PASS], BF16, "w_bf0")
-        w_lo = sb([P, 2 * K_PASS], BF16, "w_lo")
-        w_hi = sb([P, 2 * K_PASS], BF16, "w_hi")
-        w_words = [sb([P, H], U32, f"w_words{g}") for g in range(PASSES)]
-        w_planes = sb([P, H + 2 * P], U8, "w_planes")
-        w_scales = {(g, t): w_planes[4 * g : P, (t + 2 * g) * P : (t + 2 * g + 1) * P] for g in range(PASSES) for t in range(PACK)}
-        pieces = [(0, 0, 2 * P), (0, 2 * P, P), (0, 3 * P, P)] + [(t, 0, S) for t in range(1, PACK)]
-        h_ps = [psum.tile([P, width], F32, name=f"h_ps{n}", tag=f"h_ps{n}") for n, (t, s0, width) in enumerate(pieces)]
-        h = [sb([P, S], F32, f"h{t}") for t in range(PACK)]
+        picked = [sb([P, S * PACK], BF16, f"picked{g}") for g in range(PASSES)]
+        xg_words, xg_scales = {}, {}
 
-        def shared_copy(dst, src, cut):
-            if cut:
-                nc.vector.tensor_copy(out=dst[:, :cut], in_=src[:, :cut])
-            if cut < dst.shape[1]:
+        def pick(g, u, parts):
+            pairs = x_bf[g, u] = sb([P, 2 * T], BF16, f"x_pairs{g}_{u}")
+            for c0, width, share in X_CHUNKS[g, u]:
+                dst = pairs[:, 2 * c0 : 2 * (c0 + width)].rearrange("p (c i e) -> p c e i", i=4, e=2)
+                src = x_raw[g, u, c0][:].rearrange("p e (c i) -> p c e i", i=4)
+                cut = share // 4
+                if cut:
+                    nc.vector.tensor_copy(out=dst[:, :cut], in_=src[:, :cut])
                 nc.scalar.activation(out=dst[:, cut:], in_=src[:, cut:], func=COPY)
+            words = picked[g][:].bitcast(U32).rearrange("p (s u) -> p s u", u=2)
+            width = S // parts
+            for s0 in range(0, S, width):
+                nc.vector.tensor_copy(out=words[:, s0 : s0 + width, u], in_=pairs[:].bitcast(U32).indirect(offs_sb[:, s0 // 16 : (s0 + width) // 16]))
 
-        def prepare_x(g):
-            for q0, q_width in X_QUANT[g]:
-                grouped = sb([P, q_width * PACK], BF16, f"x_bf{g}_{q0}")
-                for c0, width, share in X_CHUNKS[g]:
-                    if q0 <= c0 < q0 + q_width:
-                        shared_copy(
-                            grouped[:, (c0 - q0) * PACK : (c0 - q0 + width) * PACK].rearrange("p (c i j) -> p c j i", i=2, j=PACK),
-                            x_raw[g, c0][:].rearrange("p j (c i) -> p c j i", i=2),
-                            share // 2,
-                        )
-                nc.vector.quantize_mx(
-                    out=x_words[g][:, q0 : q0 + q_width].bitcast(FP8X4),
-                    scales=x_scales[4 * g : P, q0 : q0 + q_width],
-                    in_=grouped[:],
-                )
+        def quantize_x(g, s0, width, tag=None):
+            words = sb([P, width], U32, f"xg_words{g}_{s0}", tag=tag)
+            scales = sb([P, width], U8, f"xg_scales{g}_{s0}")
+            nc.vector.quantize_mx(out=words[:].bitcast(FP8X4), scales=scales[:], in_=picked[g][:, s0 * PACK : (s0 + width) * PACK])
+            for c0 in range(0, width, HALF):
+                xg_words[g, s0 + c0] = words[:, c0 : c0 + HALF]
+                xg_scales[g, s0 + c0] = scales[:, c0 : c0 + HALF]
 
-        def round_w(g, dst, t0, tiles):
-            dealt = dst[:].rearrange("p (t m j) -> p m j t", t=tiles, j=PACK)
-            for c0, width, share in W_CHUNKS[g]:
-                shared_copy(
-                    dealt[:, c0 // 4 : (c0 + width) // 4],
-                    w_raw[g, c0][:].rearrange("p j (m t) -> p m j t", t=PACK)[:, :, :, t0 : t0 + tiles],
-                    0 if t0 else share // 4,
-                )
+        pick(0, 0, 1)
+        pick(0, 1, 1)
+        quantize_x(0, 0, S)
+        pick(1, 0, 1)
+        pick(1, 1, 2)
+        quantize_x(1, 0, HALF)
 
-        def first_product(g, n):
-            t, s0, width = pieces[n]
-            nc.tensor.matmul_mx(
-                out=h_ps[n][:],
-                lhsT=w_words[g][:, t * P : (t + 1) * P].bitcast(FP8X4),
-                lhsT_scale=w_scales[g, t],
-                rhs=xg_words[g][:, s0 : s0 + width].bitcast(FP8X4),
-                rhs_scale=xg_scales[4 * g : P, s0 : s0 + width],
-                start=(g == 0),
-                stop=(g == PASSES - 1),
-            )
+        pair_bf = {(half, g): sb([P, K_PASS], BF16, f"pair_bf{half}_{g}") for half in range(2) for g in range(PASSES)}
+        late_bf = [sb([P, 2 * K_PASS], BF16, f"late_bf{g}") for g in range(PASSES)]
+        pair_words = {key: sb([P, P], U32, f"pair_words{key[0]}_{key[1]}") for key in pair_bf}
+        pair_scales = {key: sb([P, P], U8, f"pair_scales{key[0]}_{key[1]}") for key in pair_bf}
+        late_words = [sb([P, 2 * P], U32, f"late_words{g}") for g in range(PASSES)]
+        late_scales = [sb([P, 2 * P], U8, f"late_scales{g}") for g in range(PASSES)]
 
-        prepare_x(0)
-        nc.vector.tensor_copy(out=xg_words[0][:], in_=x_words[0][:].indirect(offs_sb[:]))
-        prepare_x(1)
-        nc.vector.tensor_copy(out=xg_scales[:], in_=x_scales[:].indirect(offs_sb[:]))
-        nc.vector.tensor_copy(out=xg_words[1][:], in_=x_words[1][:].indirect(offs_sb[:]))
-        round_w(0, w_bf0, 0, PACK)
-        for t in (0, 2):
-            nc.vector.quantize_mx(
-                out=w_words[0][:, t * P : (t + 2) * P].bitcast(FP8X4),
-                scales=w_planes[:, t * P : (t + 2) * P],
-                in_=w_bf0[:, t * K_PASS : (t + 2) * K_PASS],
-            )
-        round_w(1, w_lo, 0, 2)
-        for t in range(2):
-            nc.vector.quantize_mx(
-                out=w_words[1][:, t * P : (t + 1) * P].bitcast(FP8X4), scales=w_scales[1, t], in_=w_lo[:, t * K_PASS : (t + 1) * K_PASS]
-            )
+        def w_view(half, g):
+            return w_raw[half, g][:].rearrange("p j (m t) -> p m j t", t=PACK)
 
-        def relu(n):
-            t, s0, width = pieces[n]
-            if s0:
-                nc.vector.tensor_scalar_max(out=h[t][:, s0 : s0 + width], in0=h_ps[n][:], scalar1=0.0)
+        def round_pair(half, g, on_vector=False):
+            dst = pair_bf[half, g][:].rearrange("p (m b j) -> p m j b", b=2, j=PACK)
+            if on_vector:
+                nc.vector.tensor_copy(out=dst, in_=w_view(half, g)[:, :, :, 0:2])
             else:
-                nc.scalar.activation(out=h[t][:, s0 : s0 + width], in_=h_ps[n][:], func=RELU)
+                nc.scalar.activation(out=dst, in_=w_view(half, g)[:, :, :, 0:2], func=COPY)
 
-        for g in range(PASSES):
-            for n in range(4):
-                first_product(g, n)
-        for n in range(4):
-            relu(n)
-        round_w(1, w_hi, 2, 2)
-        nc.vector.quantize_mx(out=w_words[1][:, 2 * P :].bitcast(FP8X4), scales=w_planes[4:P, H:], in_=w_hi[:])
-        for n in range(4, 6):
-            first_product(0, n)
-            first_product(1, n)
-            relu(n)
+        def round_late(half, g, on_vector=False):
+            dst = late_bf[g][:].rearrange("p (b m j) -> p m j b", b=2, j=PACK)[:, half * 64 : (half + 1) * 64]
+            if on_vector:
+                nc.vector.tensor_copy(out=dst, in_=w_view(half, g)[:, :, :, 2:4])
+            else:
+                nc.scalar.activation(out=dst, in_=w_view(half, g)[:, :, :, 2:4], func=COPY)
 
-        own, nb1, nb2 = (sb([P, PACK, V], F32, name) for name in ("own", "nb1", "nb2"))
-        for t in range(PACK):
-            for planes, offsets in ((own, cen_sb), (nb1, pos1_sb), (nb2, pos2_sb)):
-                cuts = (0, P, V) if (t == PACK - 1 and offsets is pos2_sb) else (0, V)
-                for v0, v1 in zip(cuts, cuts[1:]):
-                    nc.vector.tensor_copy(out=planes[:, t, v0:v1], in_=h[t][:].indirect(offsets[:, v0 // 16 : v1 // 16]))
+        def quantize_pair(half, g):
+            nc.vector.quantize_mx(out=pair_words[half, g][:].bitcast(FP8X4), scales=pair_scales[half, g][:], in_=pair_bf[half, g][:])
 
-        def planes_view(planes, u):
-            return planes[:, :, u * P : (u + 1) * P].rearrange("p j (c i) -> p c j i", i=4)
+        def quantize_late(g):
+            nc.vector.quantize_mx(out=late_words[g][:].bitcast(FP8X4), scales=late_scales[g][:], in_=late_bf[g][:])
+
+        round_pair(0, 0)
+        round_late(0, 0)
+        quantize_pair(0, 0)
+        quantize_x(1, HALF, HALF, tag="w_raw0_0")
+        round_pair(0, 1)
+        quantize_pair(0, 1)
+        round_late(0, 1)
+
+        h_ps = {(t, s0): psum.tile([P, HALF], F32, name=f"h_ps{t}_{s0}", tag=f"bank{2 * t + s0 // HALF}") for t in range(PACK) for s0 in (0, HALF)}
+        h = {t: sb([P, S], F32, f"h{t}") for t in range(PACK)}
+
+        def first_product(t, g):
+            if t < 2:
+                words, scales = pair_words[t, g][:], pair_scales[t, g][:]
+            else:
+                words, scales = late_words[g][:, (t - 2) * P : (t - 1) * P], late_scales[g][:, (t - 2) * P : (t - 1) * P]
+            for s0 in (0, HALF):
+                nc.tensor.matmul_mx(
+                    out=h_ps[t, s0][:],
+                    lhsT=words.bitcast(FP8X4),
+                    lhsT_scale=scales,
+                    rhs=xg_words[g, s0].bitcast(FP8X4),
+                    rhs_scale=xg_scales[g, s0],
+                    start=(g == 0),
+                    stop=(g == PASSES - 1),
+                )
+
+        def relu(t):
+            for s0 in (0, HALF):
+                nc.scalar.activation(out=h[t][:, s0 : s0 + HALF], in_=h_ps[t, s0][:], func=RELU)
+
+        first_product(0, 0)
+        first_product(0, 1)
+        relu(0)
+        round_pair(1, 0, on_vector=True)
+        round_late(1, 0, on_vector=True)
+        quantize_pair(1, 0)
+        quantize_late(0)
+        round_pair(1, 1)
+        quantize_pair(1, 1)
+        round_late(1, 1)
+        first_product(1, 0)
+        first_product(1, 1)
+        relu(1)
+
+        NB1, OWN, NB2 = range(3)
+        planes = sb([P, PACK, 3, V], BF16, "planes")
+
+        def gather(dst, t, offsets):
+            nc.vector.tensor_copy(out=dst, in_=h[t][:].indirect(offsets))
+
+        def move(half, k0, k1, src):
+            rows = slice(64 * half, 64 * half + 64)
+            nc.sync.dma_start(out=planes[rows, 0:2, k0:k1, :].rearrange("p j k v -> p j (k v)"), in_=src)
+
+        first_nb1 = pair_bf[1, 0][:, :V]
+        first_rest = pair_bf[1, 1]
+        gather(first_nb1, 0, pos1_sb[:])
+        move(0, NB1, OWN, first_nb1)
+        gather(first_rest[:, :V], 0, cen_sb[:])
+        quantize_late(1)
+        gather(first_rest[:, V:], 0, pos2_sb[:])
+        move(0, OWN, 3, first_rest[:])
+        for t in (2, 3):
+            for g in range(PASSES):
+                first_product(t, g)
+            relu(t)
+
+        second = sb([P, 3 * V], BF16, "second")
+        for k, offsets in enumerate((pos1_sb, cen_sb, pos2_sb)):
+            gather(second[:, k * V : (k + 1) * V], 1, offsets[:])
+        move(1, 0, 3, second[:])
+
+        for t in (2, 3):
+            gather(planes[:, t, OWN, :], t, cen_sb[:])
+        for t in (2, 3):
+            gather(planes[:, t, NB1, :], t, pos1_sb[:])
+            cuts = (0, P, V) if t == PACK - 1 else (0, V)
+            for v0, v1 in zip(cuts, cuts[1:]):
+                gather(planes[:, t, NB2, v0:v1], t, pos2_sb[:, v0 // 16 : v1 // 16])
+
+        def planes_view(k, u):
+            return planes[:, :, k, u * P : (u + 1) * P].rearrange("p j (c i) -> p c j i", i=4)
 
         def grouped_view(grouped):
             return grouped[:].rearrange("p (c i j) -> p c j i", i=4, j=PACK)
@@ -188,10 +235,10 @@ def tile_picked_sagecat_max_e_kernel(tc, xT, w1, w2_words, w2_scales, w3_words, 
             nc.vector.quantize_mx(out=a_words[a, u][:].bitcast(FP8X4), scales=a_scales[a, u][:], in_=(c_bf, z_bf)[a][u][:])
 
         def largest(u):
-            nc.vector.tensor_tensor(out=grouped_view(z_bf[u]), in0=planes_view(nb1, u), in1=planes_view(nb2, u), op=MAX)
+            nc.vector.tensor_tensor(out=grouped_view(z_bf[u]), in0=planes_view(NB1, u), in1=planes_view(NB2, u), op=MAX)
 
         for u in range(2):
-            nc.scalar.activation(out=grouped_view(c_bf[u]), in_=planes_view(own, u), func=COPY)
+            nc.scalar.activation(out=grouped_view(c_bf[u]), in_=planes_view(OWN, u), func=COPY)
         largest(0)
         quantize(0, 0)
         largest(1)
@@ -199,7 +246,7 @@ def tile_picked_sagecat_max_e_kernel(tc, xT, w1, w2_words, w2_scales, w3_words, 
         quantize(0, 1)
         quantize(1, 1)
 
-        o_ps = {(u, b): psum.tile([P, P], F32, name=f"o_ps{u}_{b}", tag=f"h_ps{2 * u + b}") for u in range(2) for b in range(N // P)}
+        o_ps = {(u, b): psum.tile([P, P], F32, name=f"o_ps{u}_{b}", tag=f"bank{2 * u + b}") for u in range(2) for b in range(N // P)}
         for u in range(2):
             for a in range(2):
                 for b in range(N // P):

@@ -24,9 +24,9 @@ HALF = H // 2
 
 X_CHUNKS = {
     (0, 0): [(0, 512, 256), (512, 512, 320)],
-    (0, 1): [(0, 512, 0), (512, 512, 320)],
-    (1, 0): [(0, 512, 0), (512, 512, 192)],
-    (1, 1): [(0, 512, 0), (512, 384, 256), (896, 128, 0)],
+    (0, 1): [(0, 512, 0), (512, 384, 384), (896, 128, 0)],
+    (1, 0): [(0, 512, 0), (512, 384, 384), (896, 128, 0)],
+    (1, 1): [(0, 512, 0), (512, 384, 384), (896, 128, 0)],
 }
 
 
@@ -66,8 +66,8 @@ def tile_picked_sagecat_max_e_kernel(tc, xT, w1, w2_words, w2_scales, w3_words, 
                 w_raw[half, g] = load(w1, g, 0, PACK, half * HALF, HALF, f"w_raw{half}_{g}")
             if half == 0:
                 nc.sync.dma_start(pos1_sb[:], pos1)
-                nc.sync.dma_start(pos2_sb[:], pos2)
-                nc.sync.dma_start(cen_sb[:], cen)
+        nc.sync.dma_start(cen_sb[:], cen)
+        nc.sync.dma_start(pos2_sb[:], pos2)
         w23_words = [sb([P, N], U32, f"w23_words{a}") for a in range(2)]
         for a, (words, scales) in enumerate(((w2_words, w2_scales), (w3_words, w3_scales))):
             nc.sync.dma_start(out=w23_words[a][:].bitcast(I32), in_=words[0].rearrange("p n t -> p (n t)").bitcast(I32))
@@ -80,7 +80,7 @@ def tile_picked_sagecat_max_e_kernel(tc, xT, w1, w2_words, w2_scales, w3_words, 
         picked = [sb([P, S * PACK], BF16, f"picked{g}") for g in range(PASSES)]
         xg_words, xg_scales = {}, {}
 
-        def pick(g, u, parts):
+        def round_x(g, u):
             pairs = x_bf[g, u] = sb([P, 2 * T], BF16, f"x_pairs{g}_{u}")
             for c0, width, share in X_CHUNKS[g, u]:
                 dst = pairs[:, 2 * c0 : 2 * (c0 + width)].rearrange("p (c i e) -> p c e i", i=4, e=2)
@@ -88,7 +88,11 @@ def tile_picked_sagecat_max_e_kernel(tc, xT, w1, w2_words, w2_scales, w3_words, 
                 cut = share // 4
                 if cut:
                     nc.vector.tensor_copy(out=dst[:, :cut], in_=src[:, :cut])
-                nc.scalar.activation(out=dst[:, cut:], in_=src[:, cut:], func=COPY)
+                if share < width:
+                    nc.scalar.activation(out=dst[:, cut:], in_=src[:, cut:], func=COPY)
+
+        def pick(g, u, parts):
+            pairs = x_bf[g, u]
             words = picked[g][:].bitcast(U32).rearrange("p (s u) -> p s u", u=2)
             width = S // parts
             for s0 in range(0, S, width):
@@ -102,10 +106,15 @@ def tile_picked_sagecat_max_e_kernel(tc, xT, w1, w2_words, w2_scales, w3_words, 
                 xg_words[g, s0 + c0] = words[:, c0 : c0 + HALF]
                 xg_scales[g, s0 + c0] = scales[:, c0 : c0 + HALF]
 
+        round_x(0, 0)
         pick(0, 0, 1)
+        round_x(0, 1)
         pick(0, 1, 1)
-        quantize_x(0, 0, S)
+        round_x(1, 0)
+        quantize_x(0, 0, HALF, tag="x_raw1_0_0")
         pick(1, 0, 1)
+        round_x(1, 1)
+        quantize_x(0, HALF, HALF, tag="x_raw1_1_0")
         pick(1, 1, 2)
         quantize_x(1, 0, HALF)
 
@@ -224,42 +233,39 @@ def tile_picked_sagecat_max_e_kernel(tc, xT, w1, w2_words, w2_scales, w3_words, 
             return planes[:, :, k, u * P : (u + 1) * P].rearrange("p j (c i) -> p c j i", i=4)
 
         def grouped_view(grouped):
-            return grouped[:].rearrange("p (c i j) -> p c j i", i=4, j=PACK)
+            return grouped.rearrange("p (c i j) -> p c j i", i=4, j=PACK)
 
-        c_bf = [sb([P, K_PASS], BF16, f"c_bf{u}") for u in range(2)]
-        z_bf = [sb([P, K_PASS], BF16, f"z_bf{u}") for u in range(2)]
-        a_words = {(a, u): sb([P, P], U32, f"a_words{a}_{u}") for a in range(2) for u in range(2)}
-        a_scales = {(a, u): sb([P, P], U8, f"a_scales{a}_{u}") for a in range(2) for u in range(2)}
+        c_bf = sb([P, 2 * K_PASS], BF16, "c_bf")
+        z_bf = [sb([P, K_PASS], BF16, "z_bf0")[:], c_bf[:, :K_PASS]]
+        z_plain = sb([P, PACK, P], BF16, "z_plain")
+        a_words = {(a, u): sb([P, P], U32, f"a_words{a}_{u}")[:] for a in range(2) for u in range(2)}
+        a_scales = {(a, u): sb([P, P], U8, f"a_scales{a}_{u}")[:] for a in range(2) for u in range(2)}
 
-        def quantize(a, u):
-            nc.vector.quantize_mx(out=a_words[a, u][:].bitcast(FP8X4), scales=a_scales[a, u][:], in_=(c_bf, z_bf)[a][u][:])
+        def quantize(a, u, src):
+            nc.vector.quantize_mx(out=a_words[a, u].bitcast(FP8X4), scales=a_scales[a, u], in_=src)
 
-        def largest(u):
-            nc.vector.tensor_tensor(out=grouped_view(z_bf[u]), in0=planes_view(NB1, u), in1=planes_view(NB2, u), op=MAX)
-
+        nc.scalar.activation(out=grouped_view(c_bf[:]), in_=planes[:, :, OWN, :].rearrange("p j (c i) -> p c j i", i=4), func=COPY)
+        nc.vector.tensor_tensor(out=z_plain[:], in0=planes[:, :, NB1, :P], in1=planes[:, :, NB2, :P], op=MAX)
+        nc.scalar.activation(out=grouped_view(z_bf[0]), in_=z_plain[:].rearrange("p j (c i) -> p c j i", i=4), func=COPY)
         for u in range(2):
-            nc.scalar.activation(out=grouped_view(c_bf[u]), in_=planes_view(OWN, u), func=COPY)
-        largest(0)
-        quantize(0, 0)
-        largest(1)
-        quantize(1, 0)
-        quantize(0, 1)
-        quantize(1, 1)
+            quantize(0, u, c_bf[:, u * K_PASS : (u + 1) * K_PASS])
+        nc.vector.tensor_tensor(out=grouped_view(z_bf[1]), in0=planes_view(NB1, 1), in1=planes_view(NB2, 1), op=MAX)
+        for u in range(2):
+            quantize(1, u, z_bf[u])
 
         o_ps = {(u, b): psum.tile([P, P], F32, name=f"o_ps{u}_{b}", tag=f"bank{2 * u + b}") for u in range(2) for b in range(N // P)}
-        for u in range(2):
-            for a in range(2):
-                for b in range(N // P):
-                    cols = slice(b * P, (b + 1) * P)
-                    nc.tensor.matmul_mx(
-                        out=o_ps[u, b][:],
-                        lhsT=w23_words[a][:, cols].bitcast(FP8X4),
-                        lhsT_scale=w23_scales[a][:, cols],
-                        rhs=a_words[a, u][:].bitcast(FP8X4),
-                        rhs_scale=a_scales[a, u][:],
-                        start=(a == 0),
-                        stop=(a == 1),
-                    )
+        for a, u in ((0, 0), (0, 1), (1, 0), (1, 1)):
+            for b in range(N // P):
+                cols = slice(b * P, (b + 1) * P)
+                nc.tensor.matmul_mx(
+                    out=o_ps[u, b][:],
+                    lhsT=w23_words[a][:, cols].bitcast(FP8X4),
+                    lhsT_scale=w23_scales[a][:, cols],
+                    rhs=a_words[a, u].bitcast(FP8X4),
+                    rhs_scale=a_scales[a, u],
+                    start=(a == 0),
+                    stop=(a == 1),
+                )
         o_first = sb([P, N // P, P], F32, "o_first")
         for b in range(N // P):
             nc.scalar.activation(out=o_first[:, b, :], in_=o_ps[0, b][:], func=COPY)

@@ -24,10 +24,11 @@ HALF = H // 2
 
 X_CHUNKS = {
     (0, 0): [(0, 512, 256), (512, 512, 320)],
-    (0, 1): [(0, 512, 0), (512, 384, 384), (896, 128, 0)],
-    (1, 0): [(0, 512, 0), (512, 384, 384), (896, 128, 0)],
-    (1, 1): [(0, 512, 0), (512, 384, 384), (896, 128, 0)],
+    (0, 1): [(0, 512, 0), (512, 512, 320)],
+    (1, 0): [(0, 512, 0), (512, 512, 256)],
+    (1, 1): [(0, 512, 0), (512, 256, 256), (768, 256, 0)],
 }
+W_CHUNKS = {(0, 0): [(0, 64)], (0, 1): [(0, 32), (32, 32)], (1, 0): [(0, 64)], (1, 1): [(0, 64)]}
 
 
 def tile_picked_sagecat_max_e_kernel(tc, xT, w1, w2_words, w2_scales, w3_words, w3_scales, offs, cen, pos1, pos2, out):
@@ -63,11 +64,12 @@ def tile_picked_sagecat_max_e_kernel(tc, xT, w1, w2_words, w2_scales, w3_words, 
                 nc.sync.dma_start(offs_sb[:], offs)
         for half in range(2):
             for g in range(PASSES):
-                w_raw[half, g] = load(w1, g, 0, PACK, half * HALF, HALF, f"w_raw{half}_{g}")
+                for m0, count in W_CHUNKS[half, g]:
+                    w_raw[half, g, m0] = load(w1, g, 0, PACK, half * HALF + PACK * m0, PACK * count, f"w_raw{half}_{g}_{m0}")
             if half == 0:
+                nc.sync.dma_start(cen_sb[:], cen)
                 nc.sync.dma_start(pos1_sb[:], pos1)
-        nc.sync.dma_start(cen_sb[:], cen)
-        nc.sync.dma_start(pos2_sb[:], pos2)
+                nc.sync.dma_start(pos2_sb[:], pos2)
         w23_words = [sb([P, N], U32, f"w23_words{a}") for a in range(2)]
         for a, (words, scales) in enumerate(((w2_words, w2_scales), (w3_words, w3_scales))):
             nc.sync.dma_start(out=w23_words[a][:].bitcast(I32), in_=words[0].rearrange("p n t -> p (n t)").bitcast(I32))
@@ -77,7 +79,8 @@ def tile_picked_sagecat_max_e_kernel(tc, xT, w1, w2_words, w2_scales, w3_words, 
                     in_=scales[0, 4 * q : 4 * q + 4, :].bitcast(I32),
                 )
 
-        picked = [sb([P, S * PACK], BF16, f"picked{g}") for g in range(PASSES)]
+        picked = {}
+        found = [sb([P, 2, S], U32, f"found{g}") for g in range(PASSES)]
         xg_words, xg_scales = {}, {}
 
         def round_x(g, u):
@@ -92,16 +95,20 @@ def tile_picked_sagecat_max_e_kernel(tc, xT, w1, w2_words, w2_scales, w3_words, 
                     nc.scalar.activation(out=dst[:, cut:], in_=src[:, cut:], func=COPY)
 
         def pick(g, u, parts):
-            pairs = x_bf[g, u]
-            words = picked[g][:].bitcast(U32).rearrange("p (s u) -> p s u", u=2)
             width = S // parts
             for s0 in range(0, S, width):
-                nc.vector.tensor_copy(out=words[:, s0 : s0 + width, u], in_=pairs[:].bitcast(U32).indirect(offs_sb[:, s0 // 16 : (s0 + width) // 16]))
+                nc.vector.tensor_copy(out=found[g][:, u, s0 : s0 + width], in_=x_bf[g, u][:].bitcast(U32).indirect(offs_sb[:, s0 // 16 : (s0 + width) // 16]))
+
+        def weave(g, s0, tag=None):
+            picked[g, s0] = sb([P, HALF * PACK], BF16, f"picked{g}_{s0}", tag=tag)
+            dst = picked[g, s0][:].bitcast(I32).rearrange("p (c i u) -> p c u i", i=2, u=2)
+            src = found[g][:].bitcast(I32)[:, :, s0 : s0 + HALF].rearrange("p u (c i) -> p c u i", i=2)
+            nc.vector.tensor_copy(out=dst, in_=src)
 
         def quantize_x(g, s0, width, tag=None):
             words = sb([P, width], U32, f"xg_words{g}_{s0}", tag=tag)
             scales = sb([P, width], U8, f"xg_scales{g}_{s0}")
-            nc.vector.quantize_mx(out=words[:].bitcast(FP8X4), scales=scales[:], in_=picked[g][:, s0 * PACK : (s0 + width) * PACK])
+            nc.vector.quantize_mx(out=words[:].bitcast(FP8X4), scales=scales[:], in_=picked[g, s0][:])
             for c0 in range(0, width, HALF):
                 xg_words[g, s0 + c0] = words[:, c0 : c0 + HALF]
                 xg_scales[g, s0 + c0] = scales[:, c0 : c0 + HALF]
@@ -109,13 +116,17 @@ def tile_picked_sagecat_max_e_kernel(tc, xT, w1, w2_words, w2_scales, w3_words, 
         round_x(0, 0)
         pick(0, 0, 1)
         round_x(0, 1)
-        pick(0, 1, 1)
+        pick(0, 1, 2)
+        weave(0, 0)
+        weave(0, HALF)
         round_x(1, 0)
         quantize_x(0, 0, HALF, tag="x_raw1_0_0")
         pick(1, 0, 1)
         round_x(1, 1)
         quantize_x(0, HALF, HALF, tag="x_raw1_1_0")
         pick(1, 1, 2)
+        weave(1, 0)
+        weave(1, HALF)
         quantize_x(1, 0, HALF)
 
         pair_bf = {(half, g): sb([P, K_PASS], BF16, f"pair_bf{half}_{g}") for half in range(2) for g in range(PASSES)}
@@ -125,22 +136,21 @@ def tile_picked_sagecat_max_e_kernel(tc, xT, w1, w2_words, w2_scales, w3_words, 
         late_words = [sb([P, 2 * P], U32, f"late_words{g}") for g in range(PASSES)]
         late_scales = [sb([P, 2 * P], U8, f"late_scales{g}") for g in range(PASSES)]
 
-        def w_view(half, g):
-            return w_raw[half, g][:].rearrange("p j (m t) -> p m j t", t=PACK)
-
-        def round_pair(half, g, on_vector=False):
-            dst = pair_bf[half, g][:].rearrange("p (m b j) -> p m j b", b=2, j=PACK)
+        def round_w(dst, half, g, m0, m1, t0, on_vector):
+            first = max(start for start, count in W_CHUNKS[half, g] if start <= m0)
+            src = w_raw[half, g, first][:].rearrange("p j (m t) -> p m j t", t=PACK)[:, m0 - first : m1 - first, :, t0 : t0 + 2]
             if on_vector:
-                nc.vector.tensor_copy(out=dst, in_=w_view(half, g)[:, :, :, 0:2])
+                nc.vector.tensor_copy(out=dst, in_=src)
             else:
-                nc.scalar.activation(out=dst, in_=w_view(half, g)[:, :, :, 0:2], func=COPY)
+                nc.scalar.activation(out=dst, in_=src, func=COPY)
 
-        def round_late(half, g, on_vector=False):
-            dst = late_bf[g][:].rearrange("p (b m j) -> p m j b", b=2, j=PACK)[:, half * 64 : (half + 1) * 64]
-            if on_vector:
-                nc.vector.tensor_copy(out=dst, in_=w_view(half, g)[:, :, :, 2:4])
-            else:
-                nc.scalar.activation(out=dst, in_=w_view(half, g)[:, :, :, 2:4], func=COPY)
+        def round_pair(half, g, m0=0, m1=64, on_vector=False):
+            dst = pair_bf[half, g][:].rearrange("p (m b j) -> p m j b", b=2, j=PACK)[:, m0:m1]
+            round_w(dst, half, g, m0, m1, 0, on_vector)
+
+        def round_late(half, g, m0=0, m1=64, on_vector=False):
+            dst = late_bf[g][:].rearrange("p (b m j) -> p m j b", b=2, j=PACK)
+            round_w(dst[:, half * 64 + m0 : half * 64 + m1], half, g, m0, m1, 2, on_vector)
 
         def quantize_pair(half, g):
             nc.vector.quantize_mx(out=pair_words[half, g][:].bitcast(FP8X4), scales=pair_scales[half, g][:], in_=pair_bf[half, g][:])
@@ -149,12 +159,15 @@ def tile_picked_sagecat_max_e_kernel(tc, xT, w1, w2_words, w2_scales, w3_words, 
             nc.vector.quantize_mx(out=late_words[g][:].bitcast(FP8X4), scales=late_scales[g][:], in_=late_bf[g][:])
 
         round_pair(0, 0)
-        round_late(0, 0)
         quantize_pair(0, 0)
-        quantize_x(1, HALF, HALF, tag="w_raw0_0")
-        round_pair(0, 1)
+        round_pair(0, 1, 0, 32)
+        round_pair(0, 1, 32, 64)
         quantize_pair(0, 1)
-        round_late(0, 1)
+        round_late(0, 1, 0, 32)
+        quantize_x(1, HALF, HALF, tag="w_raw0_1_0")
+        round_late(0, 0, 0, 32)
+        round_late(0, 0, 32, 64)
+        round_late(0, 1, 32, 64)
 
         h_ps = {(t, s0): psum.tile([P, HALF], F32, name=f"h_ps{t}_{s0}", tag=f"bank{2 * t + s0 // HALF}") for t in range(PACK) for s0 in (0, HALF)}
         h = {t: sb([P, S], F32, f"h{t}") for t in range(PACK)}
@@ -193,36 +206,40 @@ def tile_picked_sagecat_max_e_kernel(tc, xT, w1, w2_words, w2_scales, w3_words, 
         first_product(1, 1)
         relu(1)
 
-        NB1, OWN, NB2 = range(3)
-        planes = sb([P, PACK, 3, V], BF16, "planes")
+        NB1, NB2 = range(2)
+        c_planes = sb([P, PACK, V], BF16, "c_planes")
+        planes = sb([P, PACK, 2, V], BF16, "planes")
 
         def gather(dst, t, offsets):
             nc.vector.tensor_copy(out=dst, in_=h[t][:].indirect(offsets))
 
-        def move(half, k0, k1, src):
-            rows = slice(64 * half, 64 * half + 64)
-            nc.sync.dma_start(out=planes[rows, 0:2, k0:k1, :].rearrange("p j k v -> p j (k v)"), in_=src)
+        def move(dst, half, src):
+            nc.sync.dma_start(out=dst[64 * half : 64 * half + 64, 0:2], in_=src)
 
-        first_nb1 = pair_bf[1, 0][:, :V]
-        first_rest = pair_bf[1, 1]
-        gather(first_nb1, 0, pos1_sb[:])
-        move(0, NB1, OWN, first_nb1)
-        gather(first_rest[:, :V], 0, cen_sb[:])
+        nb_rows = planes[:].rearrange("p j k v -> p j (k v)")
+        first_own = pair_bf[1, 0][:, :V]
+        first_rest = pair_bf[1, 1][:]
+        gather(first_own, 0, cen_sb[:])
+        move(c_planes, 0, first_own)
         quantize_late(1)
+        gather(first_rest[:, :V], 0, pos1_sb[:])
         gather(first_rest[:, V:], 0, pos2_sb[:])
-        move(0, OWN, 3, first_rest[:])
+        move(nb_rows, 0, first_rest)
         for t in (2, 3):
             for g in range(PASSES):
                 first_product(t, g)
             relu(t)
 
-        second = sb([P, 3 * V], BF16, "second")
-        for k, offsets in enumerate((pos1_sb, cen_sb, pos2_sb)):
-            gather(second[:, k * V : (k + 1) * V], 1, offsets[:])
-        move(1, 0, 3, second[:])
+        second_own = sb([P, V], BF16, "second_own")
+        second_rest = sb([P, 2 * V], BF16, "second_rest")
+        gather(second_own[:], 1, cen_sb[:])
+        move(c_planes, 1, second_own[:])
+        gather(second_rest[:, :V], 1, pos1_sb[:])
+        gather(second_rest[:, V:], 1, pos2_sb[:])
+        move(nb_rows, 1, second_rest[:])
 
         for t in (2, 3):
-            gather(planes[:, t, OWN, :], t, cen_sb[:])
+            gather(c_planes[:, t, :], t, cen_sb[:])
         for t in (2, 3):
             gather(planes[:, t, NB1, :], t, pos1_sb[:])
             cuts = (0, P, V) if t == PACK - 1 else (0, V)
@@ -233,39 +250,42 @@ def tile_picked_sagecat_max_e_kernel(tc, xT, w1, w2_words, w2_scales, w3_words, 
             return planes[:, :, k, u * P : (u + 1) * P].rearrange("p j (c i) -> p c j i", i=4)
 
         def grouped_view(grouped):
-            return grouped.rearrange("p (c i j) -> p c j i", i=4, j=PACK)
+            return grouped[:].rearrange("p (c i j) -> p c j i", i=4, j=PACK)
 
-        c_bf = sb([P, 2 * K_PASS], BF16, "c_bf")
-        z_bf = [sb([P, K_PASS], BF16, "z_bf0")[:], c_bf[:, :K_PASS]]
-        z_plain = sb([P, PACK, P], BF16, "z_plain")
-        a_words = {(a, u): sb([P, P], U32, f"a_words{a}_{u}")[:] for a in range(2) for u in range(2)}
-        a_scales = {(a, u): sb([P, P], U8, f"a_scales{a}_{u}")[:] for a in range(2) for u in range(2)}
+        c_bf = [sb([P, K_PASS], BF16, f"c_bf{u}") for u in range(2)]
+        z_bf = [sb([P, K_PASS], BF16, f"z_bf{u}") for u in range(2)]
+        a_words = {(a, u): sb([P, P], U32, f"a_words{a}_{u}") for a in range(2) for u in range(2)}
+        a_scales = {(a, u): sb([P, P], U8, f"a_scales{a}_{u}") for a in range(2) for u in range(2)}
 
-        def quantize(a, u, src):
-            nc.vector.quantize_mx(out=a_words[a, u].bitcast(FP8X4), scales=a_scales[a, u], in_=src)
+        def quantize(a, u):
+            nc.vector.quantize_mx(out=a_words[a, u][:].bitcast(FP8X4), scales=a_scales[a, u][:], in_=(c_bf, z_bf)[a][u][:])
 
-        nc.scalar.activation(out=grouped_view(c_bf[:]), in_=planes[:, :, OWN, :].rearrange("p j (c i) -> p c j i", i=4), func=COPY)
-        nc.vector.tensor_tensor(out=z_plain[:], in0=planes[:, :, NB1, :P], in1=planes[:, :, NB2, :P], op=MAX)
-        nc.scalar.activation(out=grouped_view(z_bf[0]), in_=z_plain[:].rearrange("p j (c i) -> p c j i", i=4), func=COPY)
+        def largest(u):
+            nc.vector.tensor_tensor(out=grouped_view(z_bf[u]), in0=planes_view(NB1, u), in1=planes_view(NB2, u), op=MAX)
+
         for u in range(2):
-            quantize(0, u, c_bf[:, u * K_PASS : (u + 1) * K_PASS])
-        nc.vector.tensor_tensor(out=grouped_view(z_bf[1]), in0=planes_view(NB1, 1), in1=planes_view(NB2, 1), op=MAX)
-        for u in range(2):
-            quantize(1, u, z_bf[u])
+            nc.scalar.activation(out=grouped_view(c_bf[u]), in_=c_planes[:, :, u * P : (u + 1) * P].rearrange("p j (c i) -> p c j i", i=4), func=COPY)
+        largest(0)
+        quantize(0, 0)
+        largest(1)
+        quantize(1, 0)
+        quantize(0, 1)
+        quantize(1, 1)
 
         o_ps = {(u, b): psum.tile([P, P], F32, name=f"o_ps{u}_{b}", tag=f"bank{2 * u + b}") for u in range(2) for b in range(N // P)}
-        for a, u in ((0, 0), (0, 1), (1, 0), (1, 1)):
-            for b in range(N // P):
-                cols = slice(b * P, (b + 1) * P)
-                nc.tensor.matmul_mx(
-                    out=o_ps[u, b][:],
-                    lhsT=w23_words[a][:, cols].bitcast(FP8X4),
-                    lhsT_scale=w23_scales[a][:, cols],
-                    rhs=a_words[a, u].bitcast(FP8X4),
-                    rhs_scale=a_scales[a, u],
-                    start=(a == 0),
-                    stop=(a == 1),
-                )
+        for u in range(2):
+            for a in range(2):
+                for b in range(N // P):
+                    cols = slice(b * P, (b + 1) * P)
+                    nc.tensor.matmul_mx(
+                        out=o_ps[u, b][:],
+                        lhsT=w23_words[a][:, cols].bitcast(FP8X4),
+                        lhsT_scale=w23_scales[a][:, cols],
+                        rhs=a_words[a, u][:].bitcast(FP8X4),
+                        rhs_scale=a_scales[a, u][:],
+                        start=(a == 0),
+                        stop=(a == 1),
+                    )
         o_first = sb([P, N // P, P], F32, "o_first")
         for b in range(N // P):
             nc.scalar.activation(out=o_first[:, b, :], in_=o_ps[0, b][:], func=COPY)

@@ -20,15 +20,8 @@ P = 128
 PACK = 4
 K_PASS = P * PACK
 PASSES = K // K_PASS
-HALF = H // 2
-
-X_CHUNKS = {
-    (0, 0): [(0, 512, 256), (512, 512, 320)],
-    (0, 1): [(0, 512, 0), (512, 512, 320)],
-    (1, 0): [(0, 512, 0), (512, 512, 256)],
-    (1, 1): [(0, 512, 0), (512, 256, 256), (768, 256, 0)],
-}
-W_CHUNKS = {(0, 0): [(0, 64)], (0, 1): [(0, 32), (32, 32)], (1, 0): [(0, 64)], (1, 1): [(0, 64)]}
+HALF = S // 2
+SCALAR_WHOLE = [(1, 0), (1, 1)]
 
 
 def tile_picked_sagecat_max_e_kernel(tc, xT, w1, w2_words, w2_scales, w3_words, w3_scales, offs, cen, pos1, pos2, out):
@@ -49,23 +42,19 @@ def tile_picked_sagecat_max_e_kernel(tc, xT, w1, w2_words, w2_scales, w3_words, 
         for a in range(2):
             nc.vector.memset(w23_scales[a][:].bitcast(I32), 0)
 
-        x_raw, w_raw, x_bf = {}, {}, {}
-
-        def load(src, g, j0, rows, c0, width, name):
-            view = src[g * K_PASS : (g + 1) * K_PASS, :].rearrange("(p j) c -> p j c", j=PACK)
-            raw = sb([P, rows, width], F32, name)
-            nc.sync.dma_start(out=raw[:], in_=view[:, j0 : j0 + rows, c0 : c0 + width])
-            return raw
-
-        for (g, u), chunks in X_CHUNKS.items():
-            for c0, width, share in chunks:
-                x_raw[g, u, c0] = load(xT, g, 2 * u, 2, c0, width, f"x_raw{g}_{u}_{c0}")
-            if (g, u) == (0, 0):
-                nc.sync.dma_start(offs_sb[:], offs)
+        x_raw, w_raw = {}, {}
+        for g in range(PASSES):
+            rows = xT[g * K_PASS : (g + 1) * K_PASS, :].rearrange("(p j) c -> p j c", j=PACK)
+            for j in range(PACK):
+                x_raw[g, j] = sb([P, T], F32, f"x_raw{g}_{j}")
+                nc.sync.dma_start(out=x_raw[g, j][:], in_=rows[:, j, :])
+                if (g, j) == (0, 0):
+                    nc.sync.dma_start(offs_sb[:], offs)
         for half in range(2):
             for g in range(PASSES):
-                for m0, count in W_CHUNKS[half, g]:
-                    w_raw[half, g, m0] = load(w1, g, 0, PACK, half * HALF + PACK * m0, PACK * count, f"w_raw{half}_{g}_{m0}")
+                w_raw[half, g] = sb([P, PACK, H // 2], F32, f"w_raw{half}_{g}")
+                rows = w1[g * K_PASS : (g + 1) * K_PASS, :].rearrange("(p j) c -> p j c", j=PACK)
+                nc.sync.dma_start(out=w_raw[half, g][:], in_=rows[:, :, half * (H // 2) : (half + 1) * (H // 2)])
             if half == 0:
                 nc.sync.dma_start(cen_sb[:], cen)
                 nc.sync.dma_start(pos1_sb[:], pos1)
@@ -79,212 +68,176 @@ def tile_picked_sagecat_max_e_kernel(tc, xT, w1, w2_words, w2_scales, w3_words, 
                     in_=scales[0, 4 * q : 4 * q + 4, :].bitcast(I32),
                 )
 
-        picked = {}
-        found = [sb([P, 2, S], U32, f"found{g}") for g in range(PASSES)]
-        xg_words, xg_scales = {}, {}
+        def gather(on_vector, dst, window, offsets):
+            if on_vector:
+                nc.vector.tensor_copy(out=dst, in_=window[:].indirect(offsets))
+            else:
+                nc.scalar.activation(out=dst, in_=window[:].indirect(offsets), func=COPY)
 
-        def round_x(g, u):
-            pairs = x_bf[g, u] = sb([P, 2 * T], BF16, f"x_pairs{g}_{u}")
-            for c0, width, share in X_CHUNKS[g, u]:
-                dst = pairs[:, 2 * c0 : 2 * (c0 + width)].rearrange("p (c i e) -> p c e i", i=4, e=2)
-                src = x_raw[g, u, c0][:].rearrange("p e (c i) -> p c e i", i=4)
-                cut = share // 4
-                if cut:
-                    nc.vector.tensor_copy(out=dst[:, :cut], in_=src[:, :cut])
-                if share < width:
-                    nc.scalar.activation(out=dst[:, cut:], in_=src[:, cut:], func=COPY)
+        def quantize(src, width, name):
+            words = sb([P, width], U32, name + "_words")
+            scales = sb([P, width], U8, name + "_scales")
+            nc.vector.quantize_mx(out=words[:].bitcast(FP8X4), scales=scales[:], in_=src)
+            return words, scales
 
-        def pick(g, u, parts):
-            width = S // parts
-            for s0 in range(0, S, width):
-                nc.vector.tensor_copy(out=found[g][:, u, s0 : s0 + width], in_=x_bf[g, u][:].bitcast(U32).indirect(offs_sb[:, s0 // 16 : (s0 + width) // 16]))
+        def walk_rows(planes):
+            return planes.rearrange("p j (c i) -> p c j i", i=4)
 
-        def weave(g, s0, tag=None):
-            picked[g, s0] = sb([P, HALF * PACK], BF16, f"picked{g}_{s0}", tag=tag)
-            dst = picked[g, s0][:].bitcast(I32).rearrange("p (c i u) -> p c u i", i=2, u=2)
-            src = found[g][:].bitcast(I32)[:, :, s0 : s0 + HALF].rearrange("p u (c i) -> p c u i", i=2)
-            nc.vector.tensor_copy(out=dst, in_=src)
+        def walk_grouped(grouped):
+            return grouped.rearrange("p (c i j) -> p c j i", i=4, j=PACK)
 
-        def quantize_x(g, s0, width, tag=None):
-            words = sb([P, width], U32, f"xg_words{g}_{s0}", tag=tag)
-            scales = sb([P, width], U8, f"xg_scales{g}_{s0}")
-            nc.vector.quantize_mx(out=words[:].bitcast(FP8X4), scales=scales[:], in_=picked[g, s0][:])
-            for c0 in range(0, width, HALF):
-                xg_words[g, s0 + c0] = words[:, c0 : c0 + HALF]
-                xg_scales[g, s0 + c0] = scales[:, c0 : c0 + HALF]
-
-        round_x(0, 0)
-        pick(0, 0, 1)
-        round_x(0, 1)
-        pick(0, 1, 2)
-        weave(0, 0)
-        weave(0, HALF)
-        round_x(1, 0)
-        quantize_x(0, 0, HALF, tag="x_raw1_0_0")
-        pick(1, 0, 1)
-        round_x(1, 1)
-        quantize_x(0, HALF, HALF, tag="x_raw1_1_0")
-        pick(1, 1, 2)
-        weave(1, 0)
-        weave(1, HALF)
-        quantize_x(1, 0, HALF)
+        xq = {}
+        for g in range(PASSES):
+            found = sb([P, PACK, S], BF16, f"found{g}")
+            for j in range(PACK):
+                if (g, j) in SCALAR_WHOLE:
+                    gather(False, found[:, j, :], x_raw[g, j], offs_sb[:])
+                else:
+                    gather(True, found[:, j, :HALF], x_raw[g, j], offs_sb[:, : HALF // 16])
+                    gather(False, found[:, j, HALF:], x_raw[g, j], offs_sb[:, HALF // 16 :])
+            picked = [sb([P, PACK * HALF], BF16, f"picked{g}_{s}") for s in range(2)]
+            for s in range(2):
+                nc.vector.tensor_copy(out=walk_grouped(picked[s][:]), in_=walk_rows(found[:, :, s * HALF : (s + 1) * HALF]))
+            xq[g] = (sb([P, S], U32, f"xq{g}_words"), sb([P, S], U8, f"xq{g}_scales"))
+            for s in range(2):
+                cols = slice(s * HALF, (s + 1) * HALF)
+                nc.vector.quantize_mx(out=xq[g][0][:, cols].bitcast(FP8X4), scales=xq[g][1][:, cols], in_=picked[s][:])
 
         pair_bf = {(half, g): sb([P, K_PASS], BF16, f"pair_bf{half}_{g}") for half in range(2) for g in range(PASSES)}
         late_bf = [sb([P, 2 * K_PASS], BF16, f"late_bf{g}") for g in range(PASSES)]
-        pair_words = {key: sb([P, P], U32, f"pair_words{key[0]}_{key[1]}") for key in pair_bf}
-        pair_scales = {key: sb([P, P], U8, f"pair_scales{key[0]}_{key[1]}") for key in pair_bf}
-        late_words = [sb([P, 2 * P], U32, f"late_words{g}") for g in range(PASSES)]
-        late_scales = [sb([P, 2 * P], U8, f"late_scales{g}") for g in range(PASSES)]
+        wq = {}
 
-        def round_w(dst, half, g, m0, m1, t0, on_vector):
-            first = max(start for start, count in W_CHUNKS[half, g] if start <= m0)
-            src = w_raw[half, g, first][:].rearrange("p j (m t) -> p m j t", t=PACK)[:, m0 - first : m1 - first, :, t0 : t0 + 2]
+        def round_w(dst, half, g, t0, on_vector):
+            src = w_raw[half, g][:].rearrange("p j (m t) -> p m j t", t=PACK)[:, :, :, t0 : t0 + 2]
             if on_vector:
                 nc.vector.tensor_copy(out=dst, in_=src)
             else:
                 nc.scalar.activation(out=dst, in_=src, func=COPY)
 
-        def round_pair(half, g, m0=0, m1=64, on_vector=False):
-            dst = pair_bf[half, g][:].rearrange("p (m b j) -> p m j b", b=2, j=PACK)[:, m0:m1]
-            round_w(dst, half, g, m0, m1, 0, on_vector)
+        def round_pair(half, g, on_vector):
+            round_w(pair_bf[half, g][:].rearrange("p (m b j) -> p m j b", b=2, j=PACK), half, g, 0, on_vector)
 
-        def round_late(half, g, m0=0, m1=64, on_vector=False):
+        def round_late(half, g, on_vector):
             dst = late_bf[g][:].rearrange("p (b m j) -> p m j b", b=2, j=PACK)
-            round_w(dst[:, half * 64 + m0 : half * 64 + m1], half, g, m0, m1, 2, on_vector)
+            round_w(dst[:, half * 64 : (half + 1) * 64], half, g, 2, on_vector)
 
         def quantize_pair(half, g):
-            nc.vector.quantize_mx(out=pair_words[half, g][:].bitcast(FP8X4), scales=pair_scales[half, g][:], in_=pair_bf[half, g][:])
+            words, scales = quantize(pair_bf[half, g][:], P, f"pair_q{half}_{g}")
+            wq[g, half] = (words[:], scales[:])
 
         def quantize_late(g):
-            nc.vector.quantize_mx(out=late_words[g][:].bitcast(FP8X4), scales=late_scales[g][:], in_=late_bf[g][:])
+            words, scales = quantize(late_bf[g][:], 2 * P, f"late_q{g}")
+            for i in range(2):
+                wq[g, 2 + i] = (words[:, i * P : (i + 1) * P], scales[:, i * P : (i + 1) * P])
 
-        round_pair(0, 0)
-        quantize_pair(0, 0)
-        round_pair(0, 1, 0, 32)
-        round_pair(0, 1, 32, 64)
-        quantize_pair(0, 1)
-        round_late(0, 1, 0, 32)
-        quantize_x(1, HALF, HALF, tag="w_raw0_1_0")
-        round_late(0, 0, 0, 32)
-        round_late(0, 0, 32, 64)
-        round_late(0, 1, 32, 64)
-
-        h_ps = {(t, s0): psum.tile([P, HALF], F32, name=f"h_ps{t}_{s0}", tag=f"bank{2 * t + s0 // HALF}") for t in range(PACK) for s0 in (0, HALF)}
-        h = {t: sb([P, S], F32, f"h{t}") for t in range(PACK)}
+        pieces = {0: [(0, S)], 1: [(0, S)], 2: [(0, S)], 3: [(0, S)]}
+        h_ps = {(t, s0): psum.tile([P, s1 - s0], F32, name=f"h_ps{t}_{s0}", tag=f"h_bank{t}_{s0}") for t in range(PACK) for s0, s1 in pieces[t]}
+        h = {t: sb([P, S], F32, f"h{t}", tag="w_raw1_0" if t == 0 else None) for t in range(PACK)}
 
         def first_product(t, g):
-            if t < 2:
-                words, scales = pair_words[t, g][:], pair_scales[t, g][:]
-            else:
-                words, scales = late_words[g][:, (t - 2) * P : (t - 1) * P], late_scales[g][:, (t - 2) * P : (t - 1) * P]
-            for s0 in (0, HALF):
+            for s0, s1 in pieces[t]:
                 nc.tensor.matmul_mx(
                     out=h_ps[t, s0][:],
-                    lhsT=words.bitcast(FP8X4),
-                    lhsT_scale=scales,
-                    rhs=xg_words[g, s0].bitcast(FP8X4),
-                    rhs_scale=xg_scales[g, s0],
+                    lhsT=wq[g, t][0].bitcast(FP8X4),
+                    lhsT_scale=wq[g, t][1],
+                    rhs=xq[g][0][:, s0:s1].bitcast(FP8X4),
+                    rhs_scale=xq[g][1][:, s0:s1],
                     start=(g == 0),
                     stop=(g == PASSES - 1),
                 )
 
-        def relu(t):
-            for s0 in (0, HALF):
-                nc.scalar.activation(out=h[t][:, s0 : s0 + HALF], in_=h_ps[t, s0][:], func=RELU)
+        def relu(t, piece=0, on_vector=False):
+            s0, s1 = pieces[t][piece]
+            if on_vector:
+                nc.vector.tensor_scalar_max(out=h[t][:, s0:s1], in0=h_ps[t, s0][:], scalar1=0.0)
+            else:
+                nc.scalar.activation(out=h[t][:, s0:s1], in_=h_ps[t, s0][:], func=RELU)
 
+        c_planes = sb([P, PACK, V], BF16, "c_planes")
+        n_planes = [sb([P, PACK, V], BF16, f"n_planes{d}") for d in range(2)]
+        targets = {"c": (c_planes, cen_sb), "a": (n_planes[0], pos1_sb), "b": (n_planes[1], pos2_sb)}
+
+        def fetch(on_vector, which, t, u=None, staged=None):
+            planes, offsets = targets[which]
+            if t < 2:
+                if staged is None:
+                    staged = sb([P, V], BF16, f"staged_{which}{t}")[:]
+                gather(on_vector, staged, h[t], offsets[:])
+                nc.sync.dma_start(out=planes[64 * t : 64 * t + 64, 0:2], in_=staged)
+            else:
+                v0, v1 = (0, V) if u is None else (u * P, (u + 1) * P)
+                gather(on_vector, planes[:, t, v0:v1], h[t], offsets[:, v0 // 16 : v1 // 16])
+
+        round_pair(0, 0, False)
+        round_late(0, 0, False)
+        round_pair(0, 1, False)
+        round_late(0, 1, False)
+        quantize_pair(0, 0)
+        quantize_pair(0, 1)
         first_product(0, 0)
         first_product(0, 1)
+        round_pair(1, 0, False)
         relu(0)
-        round_pair(1, 0, on_vector=True)
-        round_late(1, 0, on_vector=True)
-        quantize_pair(1, 0)
+        round_late(1, 0, True)
         quantize_late(0)
-        round_pair(1, 1)
+        quantize_pair(1, 0)
+        for t in (1, 2, 3):
+            first_product(t, 0)
+        for which in "ab":
+            fetch(False, which, 0)
+        round_pair(1, 1, True)
+        round_late(1, 1, True)
         quantize_pair(1, 1)
-        round_late(1, 1)
-        first_product(1, 0)
-        first_product(1, 1)
-        relu(1)
-
-        NB1, NB2 = range(2)
-        c_planes = sb([P, PACK, V], BF16, "c_planes")
-        planes = sb([P, PACK, 2, V], BF16, "planes")
-
-        def gather(dst, t, offsets):
-            nc.vector.tensor_copy(out=dst, in_=h[t][:].indirect(offsets))
-
-        def move(dst, half, src):
-            nc.sync.dma_start(out=dst[64 * half : 64 * half + 64, 0:2], in_=src)
-
-        nb_rows = planes[:].rearrange("p j k v -> p j (k v)")
-        first_own = pair_bf[1, 0][:, :V]
-        first_rest = pair_bf[1, 1][:]
-        gather(first_own, 0, cen_sb[:])
-        move(c_planes, 0, first_own)
         quantize_late(1)
-        gather(first_rest[:, :V], 0, pos1_sb[:])
-        gather(first_rest[:, V:], 0, pos2_sb[:])
-        move(nb_rows, 0, first_rest)
-        for t in (2, 3):
-            for g in range(PASSES):
-                first_product(t, g)
-            relu(t)
-
-        second_own = sb([P, V], BF16, "second_own")
-        second_rest = sb([P, 2 * V], BF16, "second_rest")
-        gather(second_own[:], 1, cen_sb[:])
-        move(c_planes, 1, second_own[:])
-        gather(second_rest[:, :V], 1, pos1_sb[:])
-        gather(second_rest[:, V:], 1, pos2_sb[:])
-        move(nb_rows, 1, second_rest[:])
-
-        for t in (2, 3):
-            gather(c_planes[:, t, :], t, cen_sb[:])
-        for t in (2, 3):
-            gather(planes[:, t, NB1, :], t, pos1_sb[:])
-            cuts = (0, P, V) if t == PACK - 1 else (0, V)
-            for v0, v1 in zip(cuts, cuts[1:]):
-                gather(planes[:, t, NB2, v0:v1], t, pos2_sb[:, v0 // 16 : v1 // 16])
-
-        def planes_view(k, u):
-            return planes[:, :, k, u * P : (u + 1) * P].rearrange("p j (c i) -> p c j i", i=4)
-
-        def grouped_view(grouped):
-            return grouped[:].rearrange("p (c i j) -> p c j i", i=4, j=PACK)
+        for t in (1, 2, 3):
+            first_product(t, 1)
+        fetch(True, "c", 0, staged=pair_bf[1, 1][:, :V])
+        relu(1)
 
         c_bf = [sb([P, K_PASS], BF16, f"c_bf{u}") for u in range(2)]
         z_bf = [sb([P, K_PASS], BF16, f"z_bf{u}") for u in range(2)]
-        a_words = {(a, u): sb([P, P], U32, f"a_words{a}_{u}") for a in range(2) for u in range(2)}
-        a_scales = {(a, u): sb([P, P], U8, f"a_scales{a}_{u}") for a in range(2) for u in range(2)}
-
-        def quantize(a, u):
-            nc.vector.quantize_mx(out=a_words[a, u][:].bitcast(FP8X4), scales=a_scales[a, u][:], in_=(c_bf, z_bf)[a][u][:])
+        aq = {}
 
         def largest(u):
-            nc.vector.tensor_tensor(out=grouped_view(z_bf[u]), in0=planes_view(NB1, u), in1=planes_view(NB2, u), op=MAX)
+            cols = slice(u * P, (u + 1) * P)
+            nc.vector.tensor_tensor(out=walk_grouped(z_bf[u][:]), in0=walk_rows(n_planes[0][:, :, cols]), in1=walk_rows(n_planes[1][:, :, cols]), op=MAX)
 
-        for u in range(2):
-            nc.scalar.activation(out=grouped_view(c_bf[u]), in_=c_planes[:, :, u * P : (u + 1) * P].rearrange("p j (c i) -> p c j i", i=4), func=COPY)
+        fetch(True, "a", 1)
+        fetch(False, "b", 1)
+        fetch(True, "c", 1)
+        relu(2)
+        relu(3)
+        fetch(True, "a", 2)
+        fetch(False, "c", 2)
+        fetch(True, "b", 2)
+        fetch(False, "c", 3)
+        fetch(True, "a", 3, 0)
+        fetch(True, "b", 3, 0)
+        fetch(False, "a", 3, 1)
+        fetch(False, "b", 3, 1)
         largest(0)
-        quantize(0, 0)
-        largest(1)
-        quantize(1, 0)
-        quantize(0, 1)
-        quantize(1, 1)
-
-        o_ps = {(u, b): psum.tile([P, P], F32, name=f"o_ps{u}_{b}", tag=f"bank{2 * u + b}") for u in range(2) for b in range(N // P)}
         for u in range(2):
-            for a in range(2):
+            nc.scalar.activation(out=walk_grouped(c_bf[u][:]), in_=walk_rows(c_planes[:, :, u * P : (u + 1) * P]), func=COPY)
+        largest(1)
+        aq[1, 0] = quantize(z_bf[0][:], P, "zq0")
+        aq[0, 0] = quantize(c_bf[0][:], P, "cq0")
+        aq[1, 1] = quantize(z_bf[1][:], P, "zq1")
+        aq[0, 1] = quantize(c_bf[1][:], P, "cq1")
+
+        o_banks = ["h_bank0_0", "o_bank1", "o_bank2", "o_bank3"]
+        o_ps = {(u, b): psum.tile([P, P], F32, name=f"o_ps{u}_{b}", tag=o_banks[2 * u + b]) for u in range(2) for b in range(N // P)}
+        for u, order in ((0, (1, 0)), (1, (1, 0))):
+            for a in order:
                 for b in range(N // P):
                     cols = slice(b * P, (b + 1) * P)
                     nc.tensor.matmul_mx(
                         out=o_ps[u, b][:],
                         lhsT=w23_words[a][:, cols].bitcast(FP8X4),
                         lhsT_scale=w23_scales[a][:, cols],
-                        rhs=a_words[a, u][:].bitcast(FP8X4),
-                        rhs_scale=a_scales[a, u][:],
-                        start=(a == 0),
-                        stop=(a == 1),
+                        rhs=aq[a, u][0][:].bitcast(FP8X4),
+                        rhs_scale=aq[a, u][1][:],
+                        start=(a == order[0]),
+                        stop=(a == order[1]),
                     )
         o_first = sb([P, N // P, P], F32, "o_first")
         for b in range(N // P):

@@ -50,12 +50,10 @@ def tile_picked_sagecat_max_e_kernel(tc, xT, w1, w2_words, w2_scales, w3_words, 
                 nc.sync.dma_start(out=x_raw[g, j][:], in_=rows[:, j, :])
                 if (g, j) == (0, 0):
                     nc.sync.dma_start(offs_sb[:], offs)
-        for half in range(2):
-            for g in range(PASSES):
-                w_raw[half, g] = sb([P, PACK, H // 2], F32, f"w_raw{half}_{g}")
-                rows = w1[g * K_PASS : (g + 1) * K_PASS, :].rearrange("(p j) c -> p j c", j=PACK)
-                nc.sync.dma_start(out=w_raw[half, g][:], in_=rows[:, :, half * (H // 2) : (half + 1) * (H // 2)])
-            if half == 0:
+        for g in range(PASSES):
+            w_raw[g] = sb([P, PACK, H], F32, f"w_raw{g}")
+            nc.sync.dma_start(out=w_raw[g][:], in_=w1[g * K_PASS : (g + 1) * K_PASS, :].rearrange("(p j) c -> p j c", j=PACK))
+            if g == 0:
                 nc.sync.dma_start(cen_sb[:], cen)
                 nc.sync.dma_start(pos1_sb[:], pos1)
                 nc.sync.dma_start(pos2_sb[:], pos2)
@@ -97,104 +95,74 @@ def tile_picked_sagecat_max_e_kernel(tc, xT, w1, w2_words, w2_scales, w3_words, 
                     gather(False, found[:, j, HALF:], x_raw[g, j], offs_sb[:, HALF // 16 :])
             picked = [sb([P, PACK * HALF], BF16, f"picked{g}_{s}") for s in range(2)]
             for s in range(2):
-                nc.vector.tensor_copy(out=walk_grouped(picked[s][:]), in_=walk_rows(found[:, :, s * HALF : (s + 1) * HALF]))
+                if (g, s) == (1, 1):
+                    nc.scalar.copy(out=walk_grouped(picked[s][:]), in_=walk_rows(found[:, :, s * HALF : (s + 1) * HALF]))
+                else:
+                    nc.vector.tensor_copy(out=walk_grouped(picked[s][:]), in_=walk_rows(found[:, :, s * HALF : (s + 1) * HALF]))
             xq[g] = (sb([P, S], U32, f"xq{g}_words"), sb([P, S], U8, f"xq{g}_scales"))
             for s in range(2):
                 cols = slice(s * HALF, (s + 1) * HALF)
                 nc.vector.quantize_mx(out=xq[g][0][:, cols].bitcast(FP8X4), scales=xq[g][1][:, cols], in_=picked[s][:])
 
-        pair_bf = {(half, g): sb([P, K_PASS], BF16, f"pair_bf{half}_{g}") for half in range(2) for g in range(PASSES)}
-        late_bf = [sb([P, 2 * K_PASS], BF16, f"late_bf{g}") for g in range(PASSES)]
+        w_bf = {(g, a): sb([P, 2 * K_PASS], BF16, f"w_bf{g}_{a}") for g in range(PASSES) for a in range(2)}
         wq = {}
 
-        def round_w(dst, half, g, t0, on_vector):
-            src = w_raw[half, g][:].rearrange("p j (m t) -> p m j t", t=PACK)[:, :, :, t0 : t0 + 2]
+        def round_w(g, a, m0, m1, on_vector):
+            src = w_raw[g][:].rearrange("p j (m t) -> p m j t", t=PACK)[:, m0:m1, :, 2 * a : 2 * a + 2]
+            dst = w_bf[g, a][:].rearrange("p (b m j) -> p m j b", b=2, j=PACK)[:, m0:m1]
             if on_vector:
                 nc.vector.tensor_copy(out=dst, in_=src)
             else:
                 nc.scalar.activation(out=dst, in_=src, func=COPY)
 
-        def round_pair(half, g, on_vector):
-            round_w(pair_bf[half, g][:].rearrange("p (m b j) -> p m j b", b=2, j=PACK), half, g, 0, on_vector)
+        def quantize_w(g, t):
+            a, b = divmod(t, 2)
+            wq[g, t] = quantize(w_bf[g, a][:, b * K_PASS : (b + 1) * K_PASS], P, f"wq{g}_{t}")
 
-        def round_late(half, g, on_vector):
-            dst = late_bf[g][:].rearrange("p (b m j) -> p m j b", b=2, j=PACK)
-            round_w(dst[:, half * 64 : (half + 1) * 64], half, g, 2, on_vector)
-
-        def quantize_pair(half, g):
-            words, scales = quantize(pair_bf[half, g][:], P, f"pair_q{half}_{g}")
-            wq[g, half] = (words[:], scales[:])
-
-        def quantize_late(g):
-            words, scales = quantize(late_bf[g][:], 2 * P, f"late_q{g}")
-            for i in range(2):
-                wq[g, 2 + i] = (words[:, i * P : (i + 1) * P], scales[:, i * P : (i + 1) * P])
-
-        pieces = {0: [(0, S)], 1: [(0, S)], 2: [(0, S)], 3: [(0, S)]}
-        h_ps = {(t, s0): psum.tile([P, s1 - s0], F32, name=f"h_ps{t}_{s0}", tag=f"h_bank{t}_{s0}") for t in range(PACK) for s0, s1 in pieces[t]}
-        h = {t: sb([P, S], F32, f"h{t}", tag="w_raw1_0" if t == 0 else None) for t in range(PACK)}
+        h_ps = [psum.tile([P, S], F32, name=f"h_ps{t}", tag=f"h_bank{t}") for t in range(PACK)]
+        h = [sb([P, S], F32, f"h{t}") for t in range(PACK)]
 
         def first_product(t, g):
-            for s0, s1 in pieces[t]:
-                nc.tensor.matmul_mx(
-                    out=h_ps[t, s0][:],
-                    lhsT=wq[g, t][0].bitcast(FP8X4),
-                    lhsT_scale=wq[g, t][1],
-                    rhs=xq[g][0][:, s0:s1].bitcast(FP8X4),
-                    rhs_scale=xq[g][1][:, s0:s1],
-                    start=(g == 0),
-                    stop=(g == PASSES - 1),
-                )
+            nc.tensor.matmul_mx(
+                out=h_ps[t][:],
+                lhsT=wq[g, t][0][:].bitcast(FP8X4),
+                lhsT_scale=wq[g, t][1][:],
+                rhs=xq[g][0][:].bitcast(FP8X4),
+                rhs_scale=xq[g][1][:],
+                start=(g == 0),
+                stop=(g == PASSES - 1),
+            )
 
-        def relu(t, piece=0, on_vector=False):
-            s0, s1 = pieces[t][piece]
+        def relu(t, on_vector):
             if on_vector:
-                nc.vector.tensor_scalar_max(out=h[t][:, s0:s1], in0=h_ps[t, s0][:], scalar1=0.0)
+                nc.vector.tensor_scalar_max(out=h[t][:], in0=h_ps[t][:], scalar1=0.0)
             else:
-                nc.scalar.activation(out=h[t][:, s0:s1], in_=h_ps[t, s0][:], func=RELU)
+                nc.scalar.activation(out=h[t][:], in_=h_ps[t][:], func=RELU)
 
-        c_planes = sb([P, PACK, V], BF16, "c_planes")
+        c_bf = sb([P, V, PACK], BF16, "c_bf", tag="xq1_words")
         n_planes = [sb([P, PACK, V], BF16, f"n_planes{d}") for d in range(2)]
-        targets = {"c": (c_planes, cen_sb), "a": (n_planes[0], pos1_sb), "b": (n_planes[1], pos2_sb)}
 
-        def fetch(on_vector, which, t, u=None, staged=None):
-            planes, offsets = targets[which]
-            if t < 2:
-                if staged is None:
-                    staged = sb([P, V], BF16, f"staged_{which}{t}")[:]
-                gather(on_vector, staged, h[t], offsets[:])
-                nc.sync.dma_start(out=planes[64 * t : 64 * t + 64, 0:2], in_=staged)
+        def fetch(on_vector, which, t, u=None):
+            v0, v1 = (0, V) if u is None else (u * P, (u + 1) * P)
+            if which == "c":
+                gather(on_vector, c_bf[:, v0:v1, t], h[t], cen_sb[:, v0 // 16 : v1 // 16])
             else:
-                v0, v1 = (0, V) if u is None else (u * P, (u + 1) * P)
-                gather(on_vector, planes[:, t, v0:v1], h[t], offsets[:, v0 // 16 : v1 // 16])
+                d = "ab".index(which)
+                gather(on_vector, n_planes[d][:, t, v0:v1], h[t], (pos1_sb, pos2_sb)[d][:, v0 // 16 : v1 // 16])
 
-        round_pair(0, 0, False)
-        round_late(0, 0, False)
-        round_pair(0, 1, False)
-        round_late(0, 1, False)
-        quantize_pair(0, 0)
-        quantize_pair(0, 1)
-        first_product(0, 0)
-        first_product(0, 1)
-        round_pair(1, 0, False)
-        relu(0)
-        round_late(1, 0, True)
-        quantize_late(0)
-        quantize_pair(1, 0)
-        for t in (1, 2, 3):
+        round_w(0, 0, 0, P, True)
+        round_w(0, 1, 0, P, False)
+        for t in range(PACK):
+            quantize_w(0, t)
             first_product(t, 0)
-        for which in "ab":
-            fetch(False, which, 0)
-        round_pair(1, 1, True)
-        round_late(1, 1, True)
-        quantize_pair(1, 1)
-        quantize_late(1)
-        for t in (1, 2, 3):
+        round_w(1, 0, 0, 80, True)
+        round_w(1, 0, 80, P, False)
+        round_w(1, 1, 0, 64, True)
+        round_w(1, 1, 64, P, False)
+        for t in range(PACK):
+            quantize_w(1, t)
             first_product(t, 1)
-        fetch(True, "c", 0, staged=pair_bf[1, 1][:, :V])
-        relu(1)
 
-        c_bf = [sb([P, K_PASS], BF16, f"c_bf{u}") for u in range(2)]
         z_bf = [sb([P, K_PASS], BF16, f"z_bf{u}") for u in range(2)]
         aq = {}
 
@@ -202,29 +170,33 @@ def tile_picked_sagecat_max_e_kernel(tc, xT, w1, w2_words, w2_scales, w3_words, 
             cols = slice(u * P, (u + 1) * P)
             nc.vector.tensor_tensor(out=walk_grouped(z_bf[u][:]), in0=walk_rows(n_planes[0][:, :, cols]), in1=walk_rows(n_planes[1][:, :, cols]), op=MAX)
 
-        fetch(True, "a", 1)
-        fetch(False, "b", 1)
-        fetch(True, "c", 1)
-        relu(2)
-        relu(3)
+        relu(0, False)
+        relu(1, True)
+        relu(2, False)
+        relu(3, True)
+        fetch(False, "a", 0)
+        fetch(True, "b", 1)
+        fetch(False, "b", 0)
+        fetch(True, "a", 1, 1)
+        fetch(False, "a", 1, 0)
         fetch(True, "a", 2)
-        fetch(False, "c", 2)
         fetch(True, "b", 2)
-        fetch(False, "c", 3)
-        fetch(True, "a", 3, 0)
+        fetch(True, "a", 3)
         fetch(True, "b", 3, 0)
-        fetch(False, "a", 3, 1)
-        fetch(False, "b", 3, 1)
+        fetch(True, "b", 3, 1)
+        for t in range(3):
+            fetch(False, "c", t)
+        fetch(False, "c", 3, 0)
+        fetch(False, "c", 3, 1)
         largest(0)
-        for u in range(2):
-            nc.scalar.activation(out=walk_grouped(c_bf[u][:]), in_=walk_rows(c_planes[:, :, u * P : (u + 1) * P]), func=COPY)
         largest(1)
+        c_flat = c_bf[:].rearrange("p v t -> p (v t)")
         aq[1, 0] = quantize(z_bf[0][:], P, "zq0")
-        aq[0, 0] = quantize(c_bf[0][:], P, "cq0")
+        aq[0, 0] = quantize(c_flat[:, :K_PASS], P, "cq0")
         aq[1, 1] = quantize(z_bf[1][:], P, "zq1")
-        aq[0, 1] = quantize(c_bf[1][:], P, "cq1")
+        aq[0, 1] = quantize(c_flat[:, K_PASS:], P, "cq1")
 
-        o_banks = ["h_bank0_0", "o_bank1", "o_bank2", "o_bank3"]
+        o_banks = ["o_bank0", "o_bank1", "o_bank2", "o_bank3"]
         o_ps = {(u, b): psum.tile([P, P], F32, name=f"o_ps{u}_{b}", tag=o_banks[2 * u + b]) for u in range(2) for b in range(N // P)}
         for u, order in ((0, (1, 0)), (1, (1, 0))):
             for a in order:

@@ -21,7 +21,8 @@ PACK = 4
 K_PASS = P * PACK
 PASSES = K // K_PASS
 HALF = S // 2
-SCALAR_WHOLE = [(1, 0), (1, 1)]
+X_LOADS = [(0, 0, 2), (0, 2, 2), (1, 0, 1), (1, 1, 1), (1, 2, 1), (1, 3, 1)]
+X_ON_VECTOR = {(0, 0): S, (0, 1): HALF, (0, 2): S, (0, 3): 0, (1, 0): 0, (1, 1): 0, (1, 2): 384, (1, 3): HALF}
 
 
 def tile_picked_sagecat_max_e_kernel(tc, xT, w1, w2_words, w2_scales, w3_words, w3_scales, offs, cen, pos1, pos2, out):
@@ -43,20 +44,19 @@ def tile_picked_sagecat_max_e_kernel(tc, xT, w1, w2_words, w2_scales, w3_words, 
             nc.vector.memset(w23_scales[a][:].bitcast(I32), 0)
 
         x_raw, w_raw = {}, {}
-        for g in range(PASSES):
-            rows = xT[g * K_PASS : (g + 1) * K_PASS, :].rearrange("(p j) c -> p j c", j=PACK)
-            for j in range(PACK):
-                x_raw[g, j] = sb([P, T], F32, f"x_raw{g}_{j}")
-                nc.sync.dma_start(out=x_raw[g, j][:], in_=rows[:, j, :])
-                if (g, j) == (0, 0):
-                    nc.sync.dma_start(offs_sb[:], offs)
+        nc.sync.dma_start(offs_sb[:], offs)
+        for g, j0, n in X_LOADS:
+            rows = xT[g * K_PASS : (g + 1) * K_PASS, :].rearrange("(p j) c -> p (j c)", j=PACK)
+            planes = sb([P, n * T], F32, f"x_raw{g}_{j0}")
+            nc.sync.dma_start(out=planes[:], in_=rows[:, j0 * T : (j0 + n) * T])
+            for e in range(n):
+                x_raw[g, j0 + e] = planes[:, e * T : (e + 1) * T]
         for g in range(PASSES):
             w_raw[g] = sb([P, PACK, H], F32, f"w_raw{g}")
             nc.sync.dma_start(out=w_raw[g][:], in_=w1[g * K_PASS : (g + 1) * K_PASS, :].rearrange("(p j) c -> p j c", j=PACK))
-            if g == 0:
-                nc.sync.dma_start(cen_sb[:], cen)
-                nc.sync.dma_start(pos1_sb[:], pos1)
-                nc.sync.dma_start(pos2_sb[:], pos2)
+        nc.sync.dma_start(pos1_sb[:], pos1)
+        nc.sync.dma_start(pos2_sb[:], pos2)
+        nc.sync.dma_start(cen_sb[:], cen)
         w23_words = [sb([P, N], U32, f"w23_words{a}") for a in range(2)]
         for a, (words, scales) in enumerate(((w2_words, w2_scales), (w3_words, w3_scales))):
             nc.sync.dma_start(out=w23_words[a][:].bitcast(I32), in_=words[0].rearrange("p n t -> p (n t)").bitcast(I32))
@@ -68,12 +68,12 @@ def tile_picked_sagecat_max_e_kernel(tc, xT, w1, w2_words, w2_scales, w3_words, 
 
         def gather(on_vector, dst, window, offsets):
             if on_vector:
-                nc.vector.tensor_copy(out=dst, in_=window[:].indirect(offsets))
+                nc.vector.tensor_copy(out=dst, in_=window.indirect(offsets))
             else:
-                nc.scalar.activation(out=dst, in_=window[:].indirect(offsets), func=COPY)
+                nc.scalar.activation(out=dst, in_=window.indirect(offsets), func=COPY)
 
-        def quantize(src, width, name):
-            words = sb([P, width], U32, name + "_words")
+        def quantize(src, width, name, tag=None):
+            words = sb([P, width], U32, name + "_words", tag=tag)
             scales = sb([P, width], U8, name + "_scales")
             nc.vector.quantize_mx(out=words[:].bitcast(FP8X4), scales=scales[:], in_=src)
             return words, scales
@@ -86,23 +86,23 @@ def tile_picked_sagecat_max_e_kernel(tc, xT, w1, w2_words, w2_scales, w3_words, 
 
         xq = {}
         for g in range(PASSES):
-            found = sb([P, PACK, S], BF16, f"found{g}")
+            found = sb([P, PACK, S], F32 if g == 0 else BF16, f"found{g}")
             for j in range(PACK):
-                if (g, j) in SCALAR_WHOLE:
-                    gather(False, found[:, j, :], x_raw[g, j], offs_sb[:])
-                else:
-                    gather(True, found[:, j, :HALF], x_raw[g, j], offs_sb[:, : HALF // 16])
-                    gather(False, found[:, j, HALF:], x_raw[g, j], offs_sb[:, HALF // 16 :])
-            picked = [sb([P, PACK * HALF], BF16, f"picked{g}_{s}") for s in range(2)]
-            for s in range(2):
-                if (g, s) == (1, 1):
-                    nc.scalar.copy(out=walk_grouped(picked[s][:]), in_=walk_rows(found[:, :, s * HALF : (s + 1) * HALF]))
-                else:
-                    nc.vector.tensor_copy(out=walk_grouped(picked[s][:]), in_=walk_rows(found[:, :, s * HALF : (s + 1) * HALF]))
+                n = X_ON_VECTOR[g, j]
+                if n > 0:
+                    gather(True, found[:, j, :n], x_raw[g, j], offs_sb[:, : n // 16])
+                if n < S:
+                    gather(False, found[:, j, n:], x_raw[g, j], offs_sb[:, n // 16 :])
+            picked = sb([P, PACK * S], BF16, f"picked{g}")
+            cut = S if g == 0 else 320
+            nc.vector.tensor_copy(out=walk_grouped(picked[:, : PACK * HALF]), in_=walk_rows(found[:, :, :HALF]))
+            nc.vector.tensor_copy(out=walk_grouped(picked[:, PACK * HALF : PACK * cut]), in_=walk_rows(found[:, :, HALF:cut]))
+            if cut < S:
+                nc.scalar.copy(out=walk_grouped(picked[:, PACK * cut :]), in_=walk_rows(found[:, :, cut:]))
             xq[g] = (sb([P, S], U32, f"xq{g}_words"), sb([P, S], U8, f"xq{g}_scales"))
             for s in range(2):
                 cols = slice(s * HALF, (s + 1) * HALF)
-                nc.vector.quantize_mx(out=xq[g][0][:, cols].bitcast(FP8X4), scales=xq[g][1][:, cols], in_=picked[s][:])
+                nc.vector.quantize_mx(out=xq[g][0][:, cols].bitcast(FP8X4), scales=xq[g][1][:, cols], in_=picked[:, s * PACK * HALF : (s + 1) * PACK * HALF])
 
         w_bf = {(g, a): sb([P, 2 * K_PASS], BF16, f"w_bf{g}_{a}") for g in range(PASSES) for a in range(2)}
         wq = {}
@@ -119,49 +119,51 @@ def tile_picked_sagecat_max_e_kernel(tc, xT, w1, w2_words, w2_scales, w3_words, 
             a, b = divmod(t, 2)
             wq[g, t] = quantize(w_bf[g, a][:, b * K_PASS : (b + 1) * K_PASS], P, f"wq{g}_{t}")
 
-        h_ps = [psum.tile([P, S], F32, name=f"h_ps{t}", tag=f"h_bank{t}") for t in range(PACK)]
+        pieces = {0: [(0, HALF), (HALF, S)], 1: [(0, S)], 2: [(0, S)], 3: [(0, S)]}
+        h_ps = {(t, s0): psum.tile([P, s1 - s0], F32, name=f"h_ps{t}_{s0}", tag=f"h_bank{t}_{s0}") for t in range(PACK) for s0, s1 in pieces[t]}
         h = [sb([P, S], F32, f"h{t}") for t in range(PACK)]
 
         def first_product(t, g):
-            nc.tensor.matmul_mx(
-                out=h_ps[t][:],
-                lhsT=wq[g, t][0][:].bitcast(FP8X4),
-                lhsT_scale=wq[g, t][1][:],
-                rhs=xq[g][0][:].bitcast(FP8X4),
-                rhs_scale=xq[g][1][:],
-                start=(g == 0),
-                stop=(g == PASSES - 1),
-            )
+            for s0, s1 in pieces[t]:
+                nc.tensor.matmul_mx(
+                    out=h_ps[t, s0][:],
+                    lhsT=wq[g, t][0][:].bitcast(FP8X4),
+                    lhsT_scale=wq[g, t][1][:],
+                    rhs=xq[g][0][:, s0:s1].bitcast(FP8X4),
+                    rhs_scale=xq[g][1][:, s0:s1],
+                    start=(g == 0),
+                    stop=(g == PASSES - 1),
+                )
 
-        def relu(t, on_vector):
+        def relu(t, on_vector, piece=0):
+            s0, s1 = pieces[t][piece]
             if on_vector:
-                nc.vector.tensor_scalar_max(out=h[t][:], in0=h_ps[t][:], scalar1=0.0)
+                nc.vector.tensor_scalar_max(out=h[t][:, s0:s1], in0=h_ps[t, s0][:], scalar1=0.0)
             else:
-                nc.scalar.activation(out=h[t][:], in_=h_ps[t][:], func=RELU)
+                nc.scalar.activation(out=h[t][:, s0:s1], in_=h_ps[t, s0][:], func=RELU)
 
-        c_bf = sb([P, V, PACK], BF16, "c_bf", tag="xq1_words")
+        c_bf = sb([P, V, PACK], BF16, "c_bf")
         n_planes = [sb([P, PACK, V], BF16, f"n_planes{d}") for d in range(2)]
 
         def fetch(on_vector, which, t, u=None):
             v0, v1 = (0, V) if u is None else (u * P, (u + 1) * P)
             if which == "c":
-                gather(on_vector, c_bf[:, v0:v1, t], h[t], cen_sb[:, v0 // 16 : v1 // 16])
+                gather(on_vector, c_bf[:, v0:v1, t], h[t][:], cen_sb[:, v0 // 16 : v1 // 16])
             else:
                 d = "ab".index(which)
-                gather(on_vector, n_planes[d][:, t, v0:v1], h[t], (pos1_sb, pos2_sb)[d][:, v0 // 16 : v1 // 16])
+                gather(on_vector, n_planes[d][:, t, v0:v1], h[t][:], (pos1_sb, pos2_sb)[d][:, v0 // 16 : v1 // 16])
 
-        round_w(0, 0, 0, P, True)
-        round_w(0, 1, 0, P, False)
-        for t in range(PACK):
-            quantize_w(0, t)
-            first_product(t, 0)
-        round_w(1, 0, 0, 80, True)
-        round_w(1, 0, 80, P, False)
-        round_w(1, 1, 0, 64, True)
-        round_w(1, 1, 64, P, False)
-        for t in range(PACK):
-            quantize_w(1, t)
-            first_product(t, 1)
+        for g in range(PASSES):
+            round_w(g, 0, 0, 88, True)
+            round_w(g, 0, 88, P, False)
+            for t in (0, 1):
+                quantize_w(g, t)
+                first_product(t, g)
+            round_w(g, 1, 0, 64, True)
+            round_w(g, 1, 64, P, False)
+            for t in (2, 3):
+                quantize_w(g, t)
+                first_product(t, g)
 
         z_bf = [sb([P, K_PASS], BF16, f"z_bf{u}") for u in range(2)]
         aq = {}
@@ -170,20 +172,18 @@ def tile_picked_sagecat_max_e_kernel(tc, xT, w1, w2_words, w2_scales, w3_words, 
             cols = slice(u * P, (u + 1) * P)
             nc.vector.tensor_tensor(out=walk_grouped(z_bf[u][:]), in0=walk_rows(n_planes[0][:, :, cols]), in1=walk_rows(n_planes[1][:, :, cols]), op=MAX)
 
-        relu(0, False)
-        relu(1, True)
-        relu(2, False)
-        relu(3, True)
+        relu(0, False, 0)
+        relu(0, True, 1)
+        for t in (1, 2, 3):
+            relu(t, True)
         fetch(False, "a", 0)
-        fetch(True, "b", 1)
         fetch(False, "b", 0)
-        fetch(True, "a", 1, 1)
-        fetch(False, "a", 1, 0)
-        fetch(True, "a", 2)
-        fetch(True, "b", 2)
-        fetch(True, "a", 3)
-        fetch(True, "b", 3, 0)
-        fetch(True, "b", 3, 1)
+        fetch(False, "a", 1)
+        fetch(False, "b", 1, 0)
+        for t in (2, 3):
+            fetch(True, "a", t)
+            fetch(True, "b", t)
+        fetch(True, "b", 1, 1)
         for t in range(3):
             fetch(False, "c", t)
         fetch(False, "c", 3, 0)
@@ -192,11 +192,11 @@ def tile_picked_sagecat_max_e_kernel(tc, xT, w1, w2_words, w2_scales, w3_words, 
         largest(1)
         c_flat = c_bf[:].rearrange("p v t -> p (v t)")
         aq[1, 0] = quantize(z_bf[0][:], P, "zq0")
-        aq[0, 0] = quantize(c_flat[:, :K_PASS], P, "cq0")
+        aq[0, 0] = quantize(c_flat[:, :K_PASS], P, "cq0", tag="n_planes0")
         aq[1, 1] = quantize(z_bf[1][:], P, "zq1")
-        aq[0, 1] = quantize(c_flat[:, K_PASS:], P, "cq1")
+        aq[0, 1] = quantize(c_flat[:, K_PASS:], P, "cq1", tag="n_planes1")
 
-        o_banks = ["o_bank0", "o_bank1", "o_bank2", "o_bank3"]
+        o_banks = ["h_bank0_0", "o_bank1", "o_bank2", "o_bank3"]
         o_ps = {(u, b): psum.tile([P, P], F32, name=f"o_ps{u}_{b}", tag=o_banks[2 * u + b]) for u in range(2) for b in range(N // P)}
         for u, order in ((0, (1, 0)), (1, (1, 0))):
             for a in order:

@@ -85,24 +85,36 @@ def tile_picked_sagecat_max_e_kernel(tc, xT, w1, w2_words, w2_scales, w3_words, 
             return grouped.rearrange("p (c i j) -> p c j i", i=4, j=PACK)
 
         xq = {}
-        for g in range(PASSES):
-            found = sb([P, PACK, S], F32 if g == 0 else BF16, f"found{g}")
+        found_all = [sb([P, PACK, S], F32 if g == 0 else BF16, f"found{g}") for g in range(PASSES)]
+
+        def pick(g):
+            found = found_all[g]
             for j in range(PACK):
                 n = X_ON_VECTOR[g, j]
                 if n > 0:
                     gather(True, found[:, j, :n], x_raw[g, j], offs_sb[:, : n // 16])
                 if n < S:
                     gather(False, found[:, j, n:], x_raw[g, j], offs_sb[:, n // 16 :])
+
+        def pack(g):
+            found = found_all[g]
             picked = sb([P, PACK * S], BF16, f"picked{g}")
             cut = S if g == 0 else 320
             nc.vector.tensor_copy(out=walk_grouped(picked[:, : PACK * HALF]), in_=walk_rows(found[:, :, :HALF]))
             nc.vector.tensor_copy(out=walk_grouped(picked[:, PACK * HALF : PACK * cut]), in_=walk_rows(found[:, :, HALF:cut]))
             if cut < S:
                 nc.scalar.copy(out=walk_grouped(picked[:, PACK * cut :]), in_=walk_rows(found[:, :, cut:]))
-            xq[g] = (sb([P, S], U32, f"xq{g}_words"), sb([P, S], U8, f"xq{g}_scales"))
-            for s in range(2):
-                cols = slice(s * HALF, (s + 1) * HALF)
-                nc.vector.quantize_mx(out=xq[g][0][:, cols].bitcast(FP8X4), scales=xq[g][1][:, cols], in_=picked[:, s * PACK * HALF : (s + 1) * PACK * HALF])
+            if g == 0:
+                words, scales = sb([P, S], U32, "xq0_words"), sb([P, S], U8, "xq0_scales")
+                xq[0, 0, S] = (words[:], scales[:])
+                for s0 in (0, HALF):
+                    cols = slice(s0, s0 + HALF)
+                    nc.vector.quantize_mx(out=words[:, cols].bitcast(FP8X4), scales=scales[:, cols], in_=picked[:, PACK * s0 : PACK * (s0 + HALF)])
+                    xq[0, s0, s0 + HALF] = (words[:, cols], scales[:, cols])
+            else:
+                for s0, tag in ((0, None), (HALF, "w_bf0_1")):
+                    words, scales = quantize(picked[:, PACK * s0 : PACK * (s0 + HALF)], HALF, f"xq1_{s0}", tag=tag)
+                    xq[1, s0, s0 + HALF] = (words[:], scales[:])
 
         w_bf = {(g, a): sb([P, 2 * K_PASS], BF16, f"w_bf{g}_{a}") for g in range(PASSES) for a in range(2)}
         wq = {}
@@ -125,15 +137,17 @@ def tile_picked_sagecat_max_e_kernel(tc, xT, w1, w2_words, w2_scales, w3_words, 
 
         def first_product(t, g):
             for s0, s1 in pieces[t]:
-                nc.tensor.matmul_mx(
-                    out=h_ps[t, s0][:],
-                    lhsT=wq[g, t][0][:].bitcast(FP8X4),
-                    lhsT_scale=wq[g, t][1][:],
-                    rhs=xq[g][0][:, s0:s1].bitcast(FP8X4),
-                    rhs_scale=xq[g][1][:, s0:s1],
-                    start=(g == 0),
-                    stop=(g == PASSES - 1),
-                )
+                runs = [(s0, s1)] if g == 0 else [(r0, r0 + HALF) for r0 in range(s0, s1, HALF)]
+                for r0, r1 in runs:
+                    nc.tensor.matmul_mx(
+                        out=h_ps[t, s0][:, r0 - s0 : r1 - s0],
+                        lhsT=wq[g, t][0][:].bitcast(FP8X4),
+                        lhsT_scale=wq[g, t][1][:],
+                        rhs=xq[g, r0, r1][0].bitcast(FP8X4),
+                        rhs_scale=xq[g, r0, r1][1],
+                        start=(g == 0),
+                        stop=(g == PASSES - 1 and r1 == s1),
+                    )
 
         def relu(t, on_vector, piece=0):
             s0, s1 = pieces[t][piece]
@@ -145,17 +159,16 @@ def tile_picked_sagecat_max_e_kernel(tc, xT, w1, w2_words, w2_scales, w3_words, 
         c_bf = sb([P, V, PACK], BF16, "c_bf")
         n_planes = [sb([P, PACK, V], BF16, f"n_planes{d}") for d in range(2)]
 
-        def fetch(on_vector, which, t, u=None):
-            v0, v1 = (0, V) if u is None else (u * P, (u + 1) * P)
+        def fetch(on_vector, which, t, v0=0, v1=V):
             if which == "c":
                 gather(on_vector, c_bf[:, v0:v1, t], h[t][:], cen_sb[:, v0 // 16 : v1 // 16])
             else:
                 d = "ab".index(which)
                 gather(on_vector, n_planes[d][:, t, v0:v1], h[t][:], (pos1_sb, pos2_sb)[d][:, v0 // 16 : v1 // 16])
 
-        for g in range(PASSES):
-            round_w(g, 0, 0, 88, True)
-            round_w(g, 0, 88, P, False)
+        def w_pass(g):
+            round_w(g, 0, 0, 100, True)
+            round_w(g, 0, 100, P, False)
             for t in (0, 1):
                 quantize_w(g, t)
                 first_product(t, g)
@@ -164,6 +177,13 @@ def tile_picked_sagecat_max_e_kernel(tc, xT, w1, w2_words, w2_scales, w3_words, 
             for t in (2, 3):
                 quantize_w(g, t)
                 first_product(t, g)
+
+        pick(0)
+        pack(0)
+        pick(1)
+        w_pass(0)
+        pack(1)
+        w_pass(1)
 
         z_bf = [sb([P, K_PASS], BF16, f"z_bf{u}") for u in range(2)]
         aq = {}
@@ -179,15 +199,17 @@ def tile_picked_sagecat_max_e_kernel(tc, xT, w1, w2_words, w2_scales, w3_words, 
         fetch(False, "a", 0)
         fetch(False, "b", 0)
         fetch(False, "a", 1)
-        fetch(False, "b", 1, 0)
-        for t in (2, 3):
-            fetch(True, "a", t)
-            fetch(True, "b", t)
-        fetch(True, "b", 1, 1)
+        fetch(False, "b", 1, 0, 192)
+        fetch(True, "a", 2)
+        fetch(True, "b", 2)
+        fetch(True, "a", 3)
+        fetch(True, "b", 3, 0, P)
+        fetch(True, "b", 3, P, V)
+        fetch(True, "b", 1, 192, V)
         for t in range(3):
             fetch(False, "c", t)
-        fetch(False, "c", 3, 0)
-        fetch(False, "c", 3, 1)
+        fetch(False, "c", 3, 0, P)
+        fetch(False, "c", 3, P, V)
         largest(0)
         largest(1)
         c_flat = c_bf[:].rearrange("p v t -> p (v t)")

@@ -32,7 +32,7 @@ def tile_picked_sagecat_max_e_kernel(tc, xT, w1, w2_words, w2_scales, w3_words, 
         psum = ctx.enter_context(tc.psum_pool(name="psum", bufs=1))
 
         def sb(shape, dtype, name, tag=None):
-            return keep.tile(shape, dtype, name=name, tag=tag or name, align_bytes=64)
+            return keep.tile(shape, dtype, name=name, tag=tag or name, align_bytes=256)
 
         offs_sb = sb([P, S // 16], U16, "offs_sb")
         cen_sb = sb([P, V // 16], U16, "cen_sb")

@@ -21,8 +21,12 @@ PACK = 4
 K_PASS = P * PACK
 PASSES = K // K_PASS
 HALF = S // 2
+
 X_LOADS = [(0, 0, 2), (0, 2, 2), (1, 0, 1), (1, 1, 1), (1, 2, 1), (1, 3, 1)]
-X_ON_VECTOR = {(0, 0): S, (0, 1): HALF, (0, 2): S, (0, 3): 0, (1, 0): 0, (1, 1): 0, (1, 2): 384, (1, 3): HALF}
+PAIR_OF = {0: lambda j: (j % 2, j // 2), 1: lambda j: (j // 2, j % 2)}
+X_ON_VECTOR = {(0, 0): 128, (0, 1): S, (1, 0): 128, (1, 1): HALF}
+WEAVE_ON_VECTOR = {0: S, 1: HALF}
+ROUND_ON_VECTOR = {(0, 0): P, (0, 1): 0, (1, 0): 100, (1, 1): 64}
 
 
 def tile_picked_sagecat_max_e_kernel(tc, xT, w1, w2_words, w2_scales, w3_words, w3_scales, offs, cen, pos1, pos2, out):
@@ -43,17 +47,23 @@ def tile_picked_sagecat_max_e_kernel(tc, xT, w1, w2_words, w2_scales, w3_words, 
         for a in range(2):
             nc.vector.memset(w23_scales[a][:].bitcast(I32), 0)
 
-        x_raw, w_raw = {}, {}
-        nc.sync.dma_start(offs_sb[:], offs)
+        x_tile, x_raw, w_raw = {}, {}, {}
+        def load_w(g):
+            w_raw[g] = sb([P, PACK, H], F32, f"w_raw{g}")
+            nc.sync.dma_start(out=w_raw[g][:], in_=w1[g * K_PASS : (g + 1) * K_PASS, :].rearrange("(p j) c -> p j c", j=PACK))
+
         for g, j0, n in X_LOADS:
+            if (g, j0) == (1, 3):
+                load_w(0)
             rows = xT[g * K_PASS : (g + 1) * K_PASS, :].rearrange("(p j) c -> p (j c)", j=PACK)
             planes = sb([P, n * T], F32, f"x_raw{g}_{j0}")
             nc.sync.dma_start(out=planes[:], in_=rows[:, j0 * T : (j0 + n) * T])
+            if (g, j0) == (0, 0):
+                nc.sync.dma_start(offs_sb[:], offs)
+            x_tile[g, j0] = planes[:]
             for e in range(n):
                 x_raw[g, j0 + e] = planes[:, e * T : (e + 1) * T]
-        for g in range(PASSES):
-            w_raw[g] = sb([P, PACK, H], F32, f"w_raw{g}")
-            nc.sync.dma_start(out=w_raw[g][:], in_=w1[g * K_PASS : (g + 1) * K_PASS, :].rearrange("(p j) c -> p j c", j=PACK))
+        load_w(1)
         nc.sync.dma_start(pos1_sb[:], pos1)
         nc.sync.dma_start(pos2_sb[:], pos2)
         nc.sync.dma_start(cen_sb[:], cen)
@@ -78,58 +88,59 @@ def tile_picked_sagecat_max_e_kernel(tc, xT, w1, w2_words, w2_scales, w3_words, 
             nc.vector.quantize_mx(out=words[:].bitcast(FP8X4), scales=scales[:], in_=src)
             return words, scales
 
-        def walk_rows(planes):
-            return planes.rearrange("p j (c i) -> p c j i", i=4)
-
-        def walk_grouped(grouped):
-            return grouped.rearrange("p (c i j) -> p c j i", i=4, j=PACK)
+        def weave(on_vector, dst, pairs, c0, c1):
+            if on_vector:
+                nc.vector.tensor_copy(out=dst[:, PACK * c0 : PACK * c1].rearrange("p (c u e) -> p c u e", u=2, e=2), in_=pairs[:, :, c0:c1, :].rearrange("p u c e -> p c u e"))
+            else:
+                words = pairs[:].rearrange("p u c e -> p u (c e)").bitcast(U32)
+                nc.scalar.copy(out=dst[:].bitcast(U32)[:, 2 * c0 : 2 * c1].rearrange("p (c u) -> p c u", u=2), in_=words[:, :, c0:c1].rearrange("p u c -> p c u"))
 
         xq = {}
-        found_all = [sb([P, PACK, S], F32 if g == 0 else BF16, f"found{g}") for g in range(PASSES)]
+        x_pairs = [sb([P, 2, S, 2], BF16, f"x_pairs{g}") for g in range(PASSES)]
 
-        def pick(g):
-            found = found_all[g]
-            for j in range(PACK):
-                n = X_ON_VECTOR[g, j]
+        def pick(g, planes):
+            for j in planes:
+                u, e = PAIR_OF[g](j)
+                n = X_ON_VECTOR[g, u]
                 if n > 0:
-                    gather(True, found[:, j, :n], x_raw[g, j], offs_sb[:, : n // 16])
+                    gather(True, x_pairs[g][:, u, :n, e], x_raw[g, j], offs_sb[:, : n // 16])
                 if n < S:
-                    gather(False, found[:, j, n:], x_raw[g, j], offs_sb[:, n // 16 :])
+                    gather(False, x_pairs[g][:, u, n:, e], x_tile[g, j], offs_sb[:, n // 16 :])
 
         def pack(g):
-            found = found_all[g]
             picked = sb([P, PACK * S], BF16, f"picked{g}")
-            cut = S if g == 0 else 320
-            nc.vector.tensor_copy(out=walk_grouped(picked[:, : PACK * HALF]), in_=walk_rows(found[:, :, :HALF]))
-            nc.vector.tensor_copy(out=walk_grouped(picked[:, PACK * HALF : PACK * cut]), in_=walk_rows(found[:, :, HALF:cut]))
+            cut = WEAVE_ON_VECTOR[g]
+            weave(True, picked, x_pairs[g], 0, HALF)
+            if cut > HALF:
+                weave(True, picked, x_pairs[g], HALF, cut)
             if cut < S:
-                nc.scalar.copy(out=walk_grouped(picked[:, PACK * cut :]), in_=walk_rows(found[:, :, cut:]))
-            if g == 0:
-                words, scales = sb([P, S], U32, "xq0_words"), sb([P, S], U8, "xq0_scales")
-                xq[0, 0, S] = (words[:], scales[:])
-                for s0 in (0, HALF):
-                    cols = slice(s0, s0 + HALF)
-                    nc.vector.quantize_mx(out=words[:, cols].bitcast(FP8X4), scales=scales[:, cols], in_=picked[:, PACK * s0 : PACK * (s0 + HALF)])
-                    xq[0, s0, s0 + HALF] = (words[:, cols], scales[:, cols])
-            else:
-                for s0, tag in ((0, None), (HALF, "w_bf0_1")):
-                    words, scales = quantize(picked[:, PACK * s0 : PACK * (s0 + HALF)], HALF, f"xq1_{s0}", tag=tag)
-                    xq[1, s0, s0 + HALF] = (words[:], scales[:])
+                weave(False, picked, x_pairs[g], cut, S)
+            words, scales = sb([P, S], U32, f"xq{g}_words"), sb([P, S], U8, f"xq{g}_scales")
+            xq[g, 0, S] = (words[:], scales[:])
+            for s0 in (0, HALF):
+                cols = slice(s0, s0 + HALF)
+                nc.vector.quantize_mx(out=words[:, cols].bitcast(FP8X4), scales=scales[:, cols], in_=picked[:, PACK * s0 : PACK * (s0 + HALF)])
+                xq[g, s0, s0 + HALF] = (words[:, cols], scales[:, cols])
 
         w_bf = {(g, a): sb([P, 2 * K_PASS], BF16, f"w_bf{g}_{a}") for g in range(PASSES) for a in range(2)}
         wq = {}
 
         def round_w(g, a, m0, m1, on_vector):
-            src = w_raw[g][:].rearrange("p j (m t) -> p m j t", t=PACK)[:, m0:m1, :, 2 * a : 2 * a + 2]
-            dst = w_bf[g, a][:].rearrange("p (b m j) -> p m j b", b=2, j=PACK)[:, m0:m1]
+            if g == 0:
+                src = w_raw[g][:].rearrange("p (e u) (m t) -> p m e u t", u=2, t=PACK)[:, m0:m1, :, :, 2 * a : 2 * a + 2]
+                dst = w_bf[g, a][:].rearrange("p (b m u e) -> p m e u b", b=2, u=2, e=2)[:, m0:m1]
+            else:
+                src = w_raw[g][:].rearrange("p j (m t) -> p m j t", t=PACK)[:, m0:m1, :, 2 * a : 2 * a + 2]
+                dst = w_bf[g, a][:].rearrange("p (b m j) -> p m j b", b=2, j=PACK)[:, m0:m1]
             if on_vector:
                 nc.vector.tensor_copy(out=dst, in_=src)
             else:
-                nc.scalar.activation(out=dst, in_=src, func=COPY)
+                nc.scalar.copy(out=dst, in_=src)
 
         def quantize_w(g, t):
             a, b = divmod(t, 2)
-            wq[g, t] = quantize(w_bf[g, a][:, b * K_PASS : (b + 1) * K_PASS], P, f"wq{g}_{t}")
+            words, scales = quantize(w_bf[g, a][:, b * K_PASS : (b + 1) * K_PASS], P, f"wq{g}_{t}")
+            wq[g, t] = (words[:], scales[:])
 
         pieces = {0: [(0, HALF), (HALF, S)], 1: [(0, S)], 2: [(0, S)], 3: [(0, S)]}
         h_ps = {(t, s0): psum.tile([P, s1 - s0], F32, name=f"h_ps{t}_{s0}", tag=f"h_bank{t}_{s0}") for t in range(PACK) for s0, s1 in pieces[t]}
@@ -137,17 +148,15 @@ def tile_picked_sagecat_max_e_kernel(tc, xT, w1, w2_words, w2_scales, w3_words, 
 
         def first_product(t, g):
             for s0, s1 in pieces[t]:
-                runs = [(s0, s1)] if g == 0 else [(r0, r0 + HALF) for r0 in range(s0, s1, HALF)]
-                for r0, r1 in runs:
-                    nc.tensor.matmul_mx(
-                        out=h_ps[t, s0][:, r0 - s0 : r1 - s0],
-                        lhsT=wq[g, t][0][:].bitcast(FP8X4),
-                        lhsT_scale=wq[g, t][1][:],
-                        rhs=xq[g, r0, r1][0].bitcast(FP8X4),
-                        rhs_scale=xq[g, r0, r1][1],
-                        start=(g == 0),
-                        stop=(g == PASSES - 1 and r1 == s1),
-                    )
+                nc.tensor.matmul_mx(
+                    out=h_ps[t, s0][:],
+                    lhsT=wq[g, t][0].bitcast(FP8X4),
+                    lhsT_scale=wq[g, t][1],
+                    rhs=xq[g, s0, s1][0].bitcast(FP8X4),
+                    rhs_scale=xq[g, s0, s1][1],
+                    start=(g == 0),
+                    stop=(g == PASSES - 1),
+                )
 
         def relu(t, on_vector, piece=0):
             s0, s1 = pieces[t][piece]
@@ -156,32 +165,35 @@ def tile_picked_sagecat_max_e_kernel(tc, xT, w1, w2_words, w2_scales, w3_words, 
             else:
                 nc.scalar.activation(out=h[t][:, s0:s1], in_=h_ps[t, s0][:], func=RELU)
 
+        h_pairs = {which: sb([P, 2, V, 2], BF16, f"h_pairs_{which}") for which in "ab"}
+        places = {"a": pos1_sb, "b": pos2_sb, "c": cen_sb}
         c_bf = sb([P, V, PACK], BF16, "c_bf")
-        n_planes = [sb([P, PACK, V], BF16, f"n_planes{d}") for d in range(2)]
 
         def fetch(on_vector, which, t, v0=0, v1=V):
-            if which == "c":
-                gather(on_vector, c_bf[:, v0:v1, t], h[t][:], cen_sb[:, v0 // 16 : v1 // 16])
-            else:
-                d = "ab".index(which)
-                gather(on_vector, n_planes[d][:, t, v0:v1], h[t][:], (pos1_sb, pos2_sb)[d][:, v0 // 16 : v1 // 16])
+            dst = c_bf[:, v0:v1, t] if which == "c" else h_pairs[which][:, t // 2, v0:v1, t % 2]
+            gather(on_vector, dst, h[t][:], places[which][:, v0 // 16 : v1 // 16])
 
         def w_pass(g):
-            round_w(g, 0, 0, 100, True)
-            round_w(g, 0, 100, P, False)
-            for t in (0, 1):
-                quantize_w(g, t)
-                first_product(t, g)
-            round_w(g, 1, 0, 64, True)
-            round_w(g, 1, 64, P, False)
-            for t in (2, 3):
-                quantize_w(g, t)
-                first_product(t, g)
+            for a in range(2):
+                cut = ROUND_ON_VECTOR[g, a]
+                if cut > 0:
+                    round_w(g, a, 0, cut, True)
+                if cut < P:
+                    round_w(g, a, cut, P, False)
+                if (g, a) == (1, 1):
+                    words, scales = quantize(w_bf[g, a][:], 2 * P, f"wq{g}_{a}_both")
+                    for b in range(2):
+                        wq[g, 2 * a + b] = (words[:, b * P : (b + 1) * P], scales[:, b * P : (b + 1) * P])
+                for t in (2 * a, 2 * a + 1):
+                    if (g, a) != (1, 1):
+                        quantize_w(g, t)
+                    first_product(t, g)
 
-        pick(0)
+        pick(0, range(PACK))
         pack(0)
-        pick(1)
+        pick(1, range(PACK - 1))
         w_pass(0)
+        pick(1, [PACK - 1])
         pack(1)
         w_pass(1)
 
@@ -190,38 +202,37 @@ def tile_picked_sagecat_max_e_kernel(tc, xT, w1, w2_words, w2_scales, w3_words, 
 
         def largest(u):
             cols = slice(u * P, (u + 1) * P)
-            nc.vector.tensor_tensor(out=walk_grouped(z_bf[u][:]), in0=walk_rows(n_planes[0][:, :, cols]), in1=walk_rows(n_planes[1][:, :, cols]), op=MAX)
+            a_rows, b_rows = (h_pairs[which][:, :, cols, :].rearrange("p u c e -> p c u e") for which in "ab")
+            nc.vector.tensor_tensor(out=z_bf[u][:].rearrange("p (c u e) -> p c u e", u=2, e=2), in0=a_rows, in1=b_rows, op=MAX)
 
         relu(0, False, 0)
         relu(0, True, 1)
         for t in (1, 2, 3):
             relu(t, True)
-        fetch(False, "a", 0)
-        fetch(False, "b", 0)
-        fetch(False, "a", 1)
-        fetch(False, "b", 1, 0, 192)
-        fetch(True, "a", 2)
-        fetch(True, "b", 2)
-        fetch(True, "a", 3)
-        fetch(True, "b", 3, 0, P)
-        fetch(True, "b", 3, P, V)
-        fetch(True, "b", 1, 192, V)
+        for t in (0, 1):
+            fetch(False, "a", t)
+            fetch(False, "b", t, 0, 160)
+        for t in (2, 3):
+            fetch(True, "a", t)
+            fetch(True, "b", t)
+        for t in (0, 1):
+            fetch(True, "b", t, 160, V)
         for t in range(3):
             fetch(False, "c", t)
         fetch(False, "c", 3, 0, P)
         fetch(False, "c", 3, P, V)
         largest(0)
         largest(1)
-        c_flat = c_bf[:].rearrange("p v t -> p (v t)")
         aq[1, 0] = quantize(z_bf[0][:], P, "zq0")
-        aq[0, 0] = quantize(c_flat[:, :K_PASS], P, "cq0", tag="n_planes0")
+        c_flat = c_bf[:].rearrange("p v t -> p (v t)")
         aq[1, 1] = quantize(z_bf[1][:], P, "zq1")
-        aq[0, 1] = quantize(c_flat[:, K_PASS:], P, "cq1", tag="n_planes1")
+        aq[0, 0] = quantize(c_flat[:, :K_PASS], P, "cq0", tag="h_pairs_a")
+        aq[0, 1] = quantize(c_flat[:, K_PASS:], P, "cq1", tag="h_pairs_b")
 
         o_banks = ["h_bank0_0", "o_bank1", "o_bank2", "o_bank3"]
         o_ps = {(u, b): psum.tile([P, P], F32, name=f"o_ps{u}_{b}", tag=o_banks[2 * u + b]) for u in range(2) for b in range(N // P)}
-        for u, order in ((0, (1, 0)), (1, (1, 0))):
-            for a in order:
+        for u in range(2):
+            for a in (1, 0):
                 for b in range(N // P):
                     cols = slice(b * P, (b + 1) * P)
                     nc.tensor.matmul_mx(
@@ -230,8 +241,8 @@ def tile_picked_sagecat_max_e_kernel(tc, xT, w1, w2_words, w2_scales, w3_words, 
                         lhsT_scale=w23_scales[a][:, cols],
                         rhs=aq[a, u][0][:].bitcast(FP8X4),
                         rhs_scale=aq[a, u][1][:],
-                        start=(a == order[0]),
-                        stop=(a == order[1]),
+                        start=(a == 1),
+                        stop=(a == 0),
                     )
         o_first = sb([P, N // P, P], F32, "o_first")
         for b in range(N // P):

from contextlib import ExitStack

import concourse.mybir as mybir

K, T, S, V, H, N = 1024, 1024, 512, 256, 512, 256
FLOPS = 2 * K * H * S + 2 * 2 * H * N * V

F32 = mybir.dt.float32
BF16 = mybir.dt.bfloat16
I32 = mybir.dt.int32
U32 = mybir.dt.uint32
U16 = mybir.dt.uint16
U8 = mybir.dt.uint8
FP8X4 = mybir.dt.float8_e4m3fn_x4
COPY = mybir.ActivationFunctionType.Copy
RELU = mybir.ActivationFunctionType.Relu
MAX = mybir.AluOpType.max

P = 128
PACK = 4
K_PASS = P * PACK
PASSES = K // K_PASS
HALF = S // 2

X_LOADS = [(0, 0, 2), (0, 2, 2), (1, 0, 1), (1, 1, 1), (1, 2, 1), (1, 3, 1)]
PAIR_OF = {0: lambda j: (j % 2, j // 2), 1: lambda j: (j // 2, j % 2)}
X_ON_VECTOR = {(0, 0): 128, (0, 1): S, (1, 0): 128, (1, 1): HALF}
WEAVE_ON_VECTOR = {0: S, 1: HALF}
ROUND_ON_VECTOR = {(0, 0): P, (0, 1): 0, (1, 0): 100, (1, 1): 64}


def tile_picked_sagecat_max_e_kernel(tc, xT, w1, w2_words, w2_scales, w3_words, w3_scales, offs, cen, pos1, pos2, out):
    nc = tc.nc
    with ExitStack() as ctx:
        keep = ctx.enter_context(tc.tile_pool(name="keep", bufs=1))
        psum = ctx.enter_context(tc.psum_pool(name="psum", bufs=1))

        def sb(shape, dtype, name, tag=None):
            return keep.tile(shape, dtype, name=name, tag=tag or name, align_bytes=256)

        offs_sb = sb([P, S // 16], U16, "offs_sb")
        cen_sb = sb([P, V // 16], U16, "cen_sb")
        pos1_sb = sb([P, V // 16], U16, "pos1_sb")
        pos2_sb = sb([P, V // 16], U16, "pos2_sb")

        w23_scales = [sb([P, N], U8, f"w23_scales{a}") for a in range(2)]
        for a in range(2):
            nc.vector.memset(w23_scales[a][:].bitcast(I32), 0)

        x_tile, x_raw, w_raw = {}, {}, {}
        def load_w(g):
            w_raw[g] = sb([P, PACK, H], F32, f"w_raw{g}")
            nc.sync.dma_start(out=w_raw[g][:], in_=w1[g * K_PASS : (g + 1) * K_PASS, :].rearrange("(p j) c -> p j c", j=PACK))

        for g, j0, n in X_LOADS:
            if (g, j0) == (1, 3):
                load_w(0)
            rows = xT[g * K_PASS : (g + 1) * K_PASS, :].rearrange("(p j) c -> p (j c)", j=PACK)
            planes = sb([P, n * T], F32, f"x_raw{g}_{j0}")
            nc.sync.dma_start(out=planes[:], in_=rows[:, j0 * T : (j0 + n) * T])
            if (g, j0) == (0, 0):
                nc.sync.dma_start(offs_sb[:], offs)
            x_tile[g, j0] = planes[:]
            for e in range(n):
                x_raw[g, j0 + e] = planes[:, e * T : (e + 1) * T]
        load_w(1)
        nc.sync.dma_start(pos1_sb[:], pos1)
        nc.sync.dma_start(pos2_sb[:], pos2)
        nc.sync.dma_start(cen_sb[:], cen)
        w23_words = [sb([P, N], U32, f"w23_words{a}") for a in range(2)]
        for a, (words, scales) in enumerate(((w2_words, w2_scales), (w3_words, w3_scales))):
            nc.sync.dma_start(out=w23_words[a][:].bitcast(I32), in_=words[0].rearrange("p n t -> p (n t)").bitcast(I32))
            for q in range(4):
                nc.sync.dma_start(
                    out=w23_scales[a][32 * q : 32 * q + 4, :].bitcast(I32),
                    in_=scales[0, 4 * q : 4 * q + 4, :].bitcast(I32),
                )

        def gather(on_vector, dst, window, offsets):
            if on_vector:
                nc.vector.tensor_copy(out=dst, in_=window.indirect(offsets))
            else:
                nc.scalar.activation(out=dst, in_=window.indirect(offsets), func=COPY)

        def quantize(src, width, name, tag=None):
            words = sb([P, width], U32, name + "_words", tag=tag)
            scales = sb([P, width], U8, name + "_scales")
            nc.vector.quantize_mx(out=words[:].bitcast(FP8X4), scales=scales[:], in_=src)
            return words, scales

        def weave(on_vector, dst, pairs, c0, c1):
            if on_vector:
                nc.vector.tensor_copy(out=dst[:, PACK * c0 : PACK * c1].rearrange("p (c u e) -> p c u e", u=2, e=2), in_=pairs[:, :, c0:c1, :].rearrange("p u c e -> p c u e"))
            else:
                words = pairs[:].rearrange("p u c e -> p u (c e)").bitcast(U32)
                nc.scalar.copy(out=dst[:].bitcast(U32)[:, 2 * c0 : 2 * c1].rearrange("p (c u) -> p c u", u=2), in_=words[:, :, c0:c1].rearrange("p u c -> p c u"))

        xq = {}
        x_pairs = [sb([P, 2, S, 2], BF16, f"x_pairs{g}") for g in range(PASSES)]

        def pick(g, planes):
            for j in planes:
                u, e = PAIR_OF[g](j)
                n = X_ON_VECTOR[g, u]
                if n > 0:
                    gather(True, x_pairs[g][:, u, :n, e], x_raw[g, j], offs_sb[:, : n // 16])
                if n < S:
                    gather(False, x_pairs[g][:, u, n:, e], x_tile[g, j], offs_sb[:, n // 16 :])

        def pack(g):
            picked = sb([P, PACK * S], BF16, f"picked{g}")
            cut = WEAVE_ON_VECTOR[g]
            weave(True, picked, x_pairs[g], 0, HALF)
            if cut > HALF:
                weave(True, picked, x_pairs[g], HALF, cut)
            if cut < S:
                weave(False, picked, x_pairs[g], cut, S)
            words, scales = sb([P, S], U32, f"xq{g}_words"), sb([P, S], U8, f"xq{g}_scales")
            xq[g, 0, S] = (words[:], scales[:])
            for s0 in (0, HALF):
                cols = slice(s0, s0 + HALF)
                nc.vector.quantize_mx(out=words[:, cols].bitcast(FP8X4), scales=scales[:, cols], in_=picked[:, PACK * s0 : PACK * (s0 + HALF)])
                xq[g, s0, s0 + HALF] = (words[:, cols], scales[:, cols])

        w_bf = {(g, a): sb([P, 2 * K_PASS], BF16, f"w_bf{g}_{a}") for g in range(PASSES) for a in range(2)}
        wq = {}

        def round_w(g, a, m0, m1, on_vector):
            if g == 0:
                src = w_raw[g][:].rearrange("p (e u) (m t) -> p m e u t", u=2, t=PACK)[:, m0:m1, :, :, 2 * a : 2 * a + 2]
                dst = w_bf[g, a][:].rearrange("p (b m u e) -> p m e u b", b=2, u=2, e=2)[:, m0:m1]
            else:
                src = w_raw[g][:].rearrange("p j (m t) -> p m j t", t=PACK)[:, m0:m1, :, 2 * a : 2 * a + 2]
                dst = w_bf[g, a][:].rearrange("p (b m j) -> p m j b", b=2, j=PACK)[:, m0:m1]
            if on_vector:
                nc.vector.tensor_copy(out=dst, in_=src)
            else:
                nc.scalar.copy(out=dst, in_=src)

        def quantize_w(g, t):
            a, b = divmod(t, 2)
            words, scales = quantize(w_bf[g, a][:, b * K_PASS : (b + 1) * K_PASS], P, f"wq{g}_{t}")
            wq[g, t] = (words[:], scales[:])

        pieces = {0: [(0, HALF), (HALF, S)], 1: [(0, S)], 2: [(0, S)], 3: [(0, S)]}
        h_ps = {(t, s0): psum.tile([P, s1 - s0], F32, name=f"h_ps{t}_{s0}", tag=f"h_bank{t}_{s0}") for t in range(PACK) for s0, s1 in pieces[t]}
        h = [sb([P, S], F32, f"h{t}") for t in range(PACK)]

        def first_product(t, g):
            for s0, s1 in pieces[t]:
                nc.tensor.matmul_mx(
                    out=h_ps[t, s0][:],
                    lhsT=wq[g, t][0].bitcast(FP8X4),
                    lhsT_scale=wq[g, t][1],
                    rhs=xq[g, s0, s1][0].bitcast(FP8X4),
                    rhs_scale=xq[g, s0, s1][1],
                    start=(g == 0),
                    stop=(g == PASSES - 1),
                )

        def relu(t, on_vector, piece=0):
            s0, s1 = pieces[t][piece]
            if on_vector:
                nc.vector.tensor_scalar_max(out=h[t][:, s0:s1], in0=h_ps[t, s0][:], scalar1=0.0)
            else:
                nc.scalar.activation(out=h[t][:, s0:s1], in_=h_ps[t, s0][:], func=RELU)

        h_pairs = {which: sb([P, 2, V, 2], BF16, f"h_pairs_{which}") for which in "ab"}
        places = {"a": pos1_sb, "b": pos2_sb, "c": cen_sb}
        c_bf = sb([P, V, PACK], BF16, "c_bf")

        def fetch(on_vector, which, t, v0=0, v1=V):
            dst = c_bf[:, v0:v1, t] if which == "c" else h_pairs[which][:, t // 2, v0:v1, t % 2]
            gather(on_vector, dst, h[t][:], places[which][:, v0 // 16 : v1 // 16])

        def w_pass(g):
            for a in range(2):
                cut = ROUND_ON_VECTOR[g, a]
                if cut > 0:
                    round_w(g, a, 0, cut, True)
                if cut < P:
                    round_w(g, a, cut, P, False)
                if (g, a) == (1, 1):
                    words, scales = quantize(w_bf[g, a][:], 2 * P, f"wq{g}_{a}_both")
                    for b in range(2):
                        wq[g, 2 * a + b] = (words[:, b * P : (b + 1) * P], scales[:, b * P : (b + 1) * P])
                for t in (2 * a, 2 * a + 1):
                    if (g, a) != (1, 1):
                        quantize_w(g, t)
                    first_product(t, g)

        pick(0, range(PACK))
        pack(0)
        pick(1, range(PACK - 1))
        w_pass(0)
        pick(1, [PACK - 1])
        pack(1)
        w_pass(1)

        z_bf = [sb([P, K_PASS], BF16, f"z_bf{u}") for u in range(2)]
        aq = {}

        def largest(u):
            cols = slice(u * P, (u + 1) * P)
            a_rows, b_rows = (h_pairs[which][:, :, cols, :].rearrange("p u c e -> p c u e") for which in "ab")
            nc.vector.tensor_tensor(out=z_bf[u][:].rearrange("p (c u e) -> p c u e", u=2, e=2), in0=a_rows, in1=b_rows, op=MAX)

        relu(0, False, 0)
        relu(0, True, 1)
        for t in (1, 2, 3):
            relu(t, True)
        for t in (0, 1):
            fetch(False, "a", t)
            fetch(False, "b", t, 0, 160)
        for t in (2, 3):
            fetch(True, "a", t)
            fetch(True, "b", t)
        for t in (0, 1):
            fetch(True, "b", t, 160, V)
        for t in range(3):
            fetch(False, "c", t)
        fetch(False, "c", 3, 0, P)
        fetch(False, "c", 3, P, V)
        largest(0)
        largest(1)
        aq[1, 0] = quantize(z_bf[0][:], P, "zq0")
        c_flat = c_bf[:].rearrange("p v t -> p (v t)")
        aq[1, 1] = quantize(z_bf[1][:], P, "zq1")
        aq[0, 0] = quantize(c_flat[:, :K_PASS], P, "cq0", tag="h_pairs_a")
        aq[0, 1] = quantize(c_flat[:, K_PASS:], P, "cq1", tag="h_pairs_b")

        o_banks = ["h_bank0_0", "o_bank1", "o_bank2", "o_bank3"]
        o_ps = {(u, b): psum.tile([P, P], F32, name=f"o_ps{u}_{b}", tag=o_banks[2 * u + b]) for u in range(2) for b in range(N // P)}
        for u in range(2):
            for a in (1, 0):
                for b in range(N // P):
                    cols = slice(b * P, (b + 1) * P)
                    nc.tensor.matmul_mx(
                        out=o_ps[u, b][:],
                        lhsT=w23_words[a][:, cols].bitcast(FP8X4),
                        lhsT_scale=w23_scales[a][:, cols],
                        rhs=aq[a, u][0][:].bitcast(FP8X4),
                        rhs_scale=aq[a, u][1][:],
                        start=(a == 1),
                        stop=(a == 0),
                    )
        o_first = sb([P, N // P, P], F32, "o_first")
        for b in range(N // P):
            nc.scalar.activation(out=o_first[:, b, :], in_=o_ps[0, b][:], func=COPY)
        nc.sync.dma_start(out=out[:, :P].rearrange("(b p) v -> p b v", p=P), in_=o_first[:])
        o_sb = [sb([P, P], F32, f"o_sb{b}") for b in range(N // P)]
        nc.scalar.activation(out=o_sb[0][:], in_=o_ps[1, 0][:], func=COPY)
        nc.sync.dma_start(out=out[0:P, P:], in_=o_sb[0][:])
        nc.vector.tensor_copy(out=o_sb[1][:], in_=o_ps[1, 1][:])
        nc.scalar.dma_start(out=out[P : 2 * P, P:], in_=o_sb[1][:])
